import numpy as np
import ml_dtypes


def mxq(x, axis, fmt="e4m3"):
    dtype, down = {"e4m3": (ml_dtypes.float8_e4m3fn, 7), "e5m2": (ml_dtypes.float8_e5m2, 14)}[fmt]
    v = np.moveaxis(np.asarray(x, np.float32).astype(ml_dtypes.bfloat16).astype(np.float64), axis, -1)
    blocks = v.reshape(v.shape[:-1] + (-1, 32))
    amax = np.abs(blocks).max(-1, keepdims=True)
    byte = np.maximum(np.where(amax > 0, np.frexp(amax)[1] - 1 + 127, 0) - down, 1)
    scale = np.exp2(byte - 127.0)
    codes = (blocks / scale).astype(np.float32).astype(dtype).astype(np.float64)
    return np.moveaxis((codes * scale).reshape(v.shape), -1, axis)


WIDE = False


def mx_kscale(k):
    if not WIDE:
        return np.ones(k)
    levels = np.array([10, -10, 5, -5, 0])
    if k % 512:
        return np.exp2(np.random.permutation(np.resize(levels, k // 32))).repeat(32)
    a = np.empty((k // 512, 16))
    for p in range(k // 512):
        a[p, :8] = np.random.permutation(np.resize(levels, 8))
        for g in range(8):
            far = levels[np.abs(levels - a[p, g]) >= 10]
            a[p, g + 8] = far[np.random.randint(len(far))]
    return np.exp2(a.ravel()).repeat(32)


def f64(x):
    return np.asarray(x).astype(np.float64)


def striped(idx):
    return np.tile(idx.reshape(-1, 16).T, (8, 1)).astype(np.uint16)


def unstriped(offs):
    return offs[:16].T.reshape(-1).astype(np.int64)


E2M1 = np.array([0.0, 0.5, 1.0, 1.5, 2.0, 3.0, 4.0, 6.0, -0.0, -0.5, -1.0, -1.5, -2.0, -3.0, -4.0, -6.0])


def pack_weight(w, fmt):
    k, n = w.shape
    w = f64(np.asarray(w, np.float32).astype(ml_dtypes.bfloat16)).reshape(k // 32, 32, n)
    amax = np.abs(w).max(1)
    if fmt == "e4m3":
        byte = np.frexp(amax)[1] - 1 + 127 - 7
    else:
        mant, ex = np.frexp(amax / 6.0)
        byte = np.where(mant > 0.5, ex, ex - 1) + 127
    byte = np.clip(np.where(amax > 0, byte, 1), 1, 254)
    scaled = (w * np.exp2(127.0 - byte)[:, None, :]).reshape(k, n).astype(np.float32)
    by_word = np.ascontiguousarray(scaled.reshape(k // 512, 128, 4, n).transpose(0, 1, 3, 2))
    if fmt == "e4m3":
        words = by_word.astype(ml_dtypes.float8_e4m3fn).view(np.uint8)
    else:
        c = by_word.astype(ml_dtypes.float4_e2m1fn).view(np.uint8) & 0xF
        words = (c[..., 0::2] | (c[..., 1::2] << 4)).reshape(k // 512, 128, 2 * n)
    return np.ascontiguousarray(words), np.ascontiguousarray(byte.astype(np.uint8).reshape(k // 512, 16, n))


def unpack_weight(words, scales, fmt):
    g, _, n = scales.shape
    words = np.ascontiguousarray(words).reshape(g, 128, n, -1)
    if fmt == "e4m3":
        vals = words.view(ml_dtypes.float8_e4m3fn).astype(np.float64)
    else:
        nib = np.empty((g, 128, n, 4), np.uint8)
        nib[..., 0::2] = words & 0xF
        nib[..., 1::2] = words >> 4
        vals = E2M1[nib]
    vals = vals * np.repeat(np.exp2(scales.astype(np.float64) - 127.0), 8, axis=1)[..., None]
    return vals.transpose(0, 1, 3, 2).reshape(g * 512, n)


def gelu(v):
    return 0.5 * v * (1.0 + np.tanh(np.sqrt(2.0 / np.pi) * (v + 0.044715 * v**3)))


K, T, E, C, H, N = 512, 512, 4, 256, 512, 512


def by_expert(wq, xq):
    return np.concatenate([wq[e].T @ xq[:, e * C:(e + 1) * C] for e in range(E)], axis=1)


def setup_inputs():
    n = np.random.standard_normal
    s = mx_kscale(K)
    u = mx_kscale(H)
    slot_token = np.concatenate([np.random.permutation(T)[:C] for e in range(E)])
    partner = np.concatenate([np.random.permutation(T) for _ in range(-(-E * C // T))])[:E * C]
    x = pack_weight(n((K, T)) * s[:, None], "e4m3")
    wp = [pack_weight(m, "e2m1") for m in n((E, K, H)) / np.sqrt(K) / s[None, :, None] * u]
    return {
        "x_words": x[0],
        "x_scales": x[1],
        "w1": (n((E, K, H)) / np.sqrt(K) / s[None, :, None] * u).astype(np.float32),
        "wp_words": np.stack([m[0] for m in wp]),
        "wp_scales": np.stack([m[1] for m in wp]),
        "w2": (n((E, H, N)) / np.sqrt(H) / u[None, :, None]).astype(np.float32),
        "offs": striped(slot_token),
        "offs2": striped(partner),
    }


def reference(x_words, x_scales, w1, wp_words, wp_scales, w2, offs, offs2):
    w1q = mxq(f64(w1), 1, "e4m3")
    wp = np.stack([unpack_weight(wp_words[e], wp_scales[e], "e2m1") for e in range(E)])
    w2q = mxq(f64(w2), 1, "e4m3")
    idx, idx2 = unstriped(offs), unstriped(offs2)
    x = unpack_weight(x_words, x_scales, "e4m3")
    h = gelu(by_expert(w1q, x[:, idx]) + by_expert(wp, x[:, idx2]))
    y = by_expert(w2q, mxq(h, 0, "e4m3"))
    out = y
    return out

@@ -1,0 +1,240 @@
+from contextlib import ExitStack
+
+import concourse.mybir as mybir
+
+K, T, E, C, H, N = 512, 512, 4, 256, 512, 512
+FLOPS = 2 * E * C * (2 * K * H + H * N)
+
+F32 = mybir.dt.float32
+BF16 = mybir.dt.bfloat16
+I32 = mybir.dt.int32
+U32 = mybir.dt.uint32
+U16 = mybir.dt.uint16
+U8 = mybir.dt.uint8
+FP8X4 = mybir.dt.float8_e4m3fn_x4
+FP4X4 = mybir.dt.float4_e2m1fn_x4
+GELU = mybir.ActivationFunctionType.Gelu_apprx_tanh
+
+P = 128
+PACK = 4
+M = 128
+ALIGN = 64
+LIST_COLS = C // 16
+
+W1_SCALAR = (512, 512, 512, 512)
+W2_SCALAR = (512, 0, 128, 192)
+
+
+def tile_moe_duo_s_gelu_kernel(
+    tc, x_words, x_scales, w1, wp_words, wp_scales, w2, offs, offs2, out
+):
+    nc = tc.nc
+    with ExitStack() as ctx:
+        lists = ctx.enter_context(tc.tile_pool(name="lists", bufs=1))
+        sb = ctx.enter_context(tc.tile_pool(name="sb", bufs=1))
+        psum_h = ctx.enter_context(tc.psum_pool(name="psum_h", bufs=4))
+        psum_y = ctx.enter_context(tc.psum_pool(name="psum_y", bufs=4))
+
+        def tile(shape, dtype, name, tag=None):
+            return sb.tile(shape, dtype, name=name, tag=tag or name, align_bytes=ALIGN)
+
+        token_list = lists.tile([P, E * LIST_COLS], U16, name="token_list")
+        partner_list = lists.tile([P, E * LIST_COLS], U16, name="partner_list")
+        x_codes = tile([P, T], I32, "x_codes")
+        x_plane = tile([P, T], U8, "x_plane")
+        wp_plane_raw = tile([P, E, H], U8, "wp_plane_raw")
+
+        nc.vector.memset(x_plane[:].bitcast(I32), 0)
+        nc.vector.memset(wp_plane_raw[:].bitcast(I32), 0)
+
+        nc.sync.dma_start(x_codes[:], x_words[0].rearrange("p t d -> p (t d)").bitcast(I32))
+        nc.sync.dma_start(token_list[:], offs)
+        nc.sync.dma_start(partner_list[:], offs2)
+        x_rows = x_scales[0].bitcast(I32).rearrange("(q r) c -> r q c", r=4)
+        for r in range(4):
+            nc.sync.dma_start(x_plane[:].bitcast(I32)[r:P:32, :], x_rows[r])
+        wp_rows = wp_scales.bitcast(I32).rearrange("e s (q r) c -> r q (e s) c", r=4)
+
+        raw = {}
+        wp_raw = {}
+
+        def load_matrix(name, w, e):
+            raw[name, e] = tile([P, PACK, 512], F32, "raw_%s_%d" % (name, e))
+            nc.sync.dma_start(raw[name, e][:], w[e].rearrange("(p j) c -> p j c", j=PACK))
+
+        def load_wp(e):
+            wp_raw[e] = tile([P, 2 * H], U8, "wp_raw_%d" % e)
+            nc.sync.dma_start(wp_raw[e][:].bitcast(I32), wp_words[e, 0].bitcast(I32))
+
+        load_matrix("w1", w1, 0)
+        load_wp(0)
+        for r in range(4):
+            nc.sync.dma_start(wp_plane_raw[:].bitcast(I32)[r:P:32, :, :], wp_rows[r])
+        for e in range(1, E):
+            load_matrix("w1", w1, e)
+            load_wp(e)
+            load_matrix("w2", w2, e - 1)
+        load_matrix("w2", w2, E - 1)
+
+        words = {}
+        planes = {}
+
+        def gather_words(e, tag=None):
+            words[e] = tile([P, 2, C], U32, "words_%d" % e, tag)
+            for s, lst in enumerate((token_list, partner_list)):
+                offsets = lst[:, e * LIST_COLS : (e + 1) * LIST_COLS]
+                nc.vector.tensor_copy(words[e][:, s, :], x_codes[:].bitcast(U32).indirect(offsets))
+
+        def gather_planes(e, tag=None):
+            planes[e] = tile([P, 2, C], U8, "planes_%d" % e, tag)
+            for s, lst in enumerate((token_list, partner_list)):
+                offsets = lst[:, e * LIST_COLS : (e + 1) * LIST_COLS]
+                nc.vector.tensor_copy(planes[e][:, s, :], x_plane[:].indirect(offsets))
+
+        wp_codes = {}
+        wp_plane = {}
+
+        def permute_wp(e):
+            wp_codes[e] = tile([P, 2 * H], U8, "wp_codes_%d" % e)
+            wp_plane[e] = tile([P, H], U8, "wp_plane_%d" % e)
+            nc.vector.tensor_copy(
+                wp_codes[e][:].bitcast(U16).rearrange("p (t m) -> p m t", t=PACK),
+                wp_raw[e][:].bitcast(U16).rearrange("p (m t) -> p m t", t=PACK),
+            )
+            nc.vector.tensor_copy(
+                wp_plane[e][:].rearrange("p (t m) -> p t m", t=PACK),
+                wp_plane_raw[:, e, :].rearrange("p (m t) -> p t m", t=PACK),
+            )
+
+        grouped = {}
+        codes = {}
+        scales = {}
+
+        def cast(name, e, scalar_cols):
+            grouped[name, e] = tile([P, 512 * PACK], BF16, "grouped_%s_%d" % (name, e))
+            src = raw[name, e][:].rearrange("p j (m t) -> p m j t", t=4)
+            if name == "w1":
+                dst = grouped[name, e][:].rearrange("p (t m j) -> p m j t", t=4, j=PACK)
+            else:
+                dst = grouped[name, e][:].rearrange("p (m t j) -> p m j t", t=4, j=PACK)
+            cut = scalar_cols // 4
+            if cut > 0:
+                nc.scalar.copy(dst[:, :cut], src[:, :cut])
+            if cut < 128:
+                nc.vector.tensor_copy(dst[:, cut:], src[:, cut:])
+
+        def quantize(name, e, pieces=1):
+            codes[name, e] = tile([P, 512], U32, "codes_%s_%d" % (name, e))
+            scales[name, e] = tile([P, 512], U8, "scales_%s_%d" % (name, e))
+            width = 512 // pieces
+            for i in range(pieces):
+                nc.vector.quantize_mx(
+                    out=codes[name, e][:, i * width : (i + 1) * width].bitcast(FP8X4),
+                    scales=scales[name, e][:, i * width : (i + 1) * width],
+                    in_=grouped[name, e][:, i * width * PACK : (i + 1) * width * PACK],
+                )
+
+        hidden = {}
+
+        def first_layer(e):
+            hidden[e] = tile([P, C * PACK], BF16, "hidden_%d" % e)
+            for half in range(C // M):
+                slots = slice(half * M, (half + 1) * M)
+                bank = psum_h.tile([P, PACK, M], F32, name="bank_h")
+                for t in range(PACK):
+                    cols = slice(t * M, (t + 1) * M)
+                    nc.tensor.matmul_mx(
+                        out=bank[:, t, :],
+                        lhsT=codes["w1", e][:, cols].bitcast(FP8X4),
+                        lhsT_scale=scales["w1", e][:, cols],
+                        rhs=words[e][:, 0, slots].bitcast(FP8X4),
+                        rhs_scale=planes[e][:, 0, slots],
+                        start=True,
+                        stop=False,
+                    )
+                    nc.tensor.matmul_mx(
+                        out=bank[:, t, :],
+                        lhsT=wp_codes[e][:, 2 * t * M : 2 * (t + 1) * M].bitcast(FP4X4),
+                        lhsT_scale=wp_plane[e][:, cols],
+                        rhs=words[e][:, 1, slots].bitcast(FP8X4),
+                        rhs_scale=planes[e][:, 1, slots],
+                        start=False,
+                        stop=True,
+                    )
+                nc.scalar.activation(
+                    hidden[e][:, half * M * PACK : (half + 1) * M * PACK].rearrange("p (n t) -> p n t", t=PACK),
+                    bank[:].rearrange("p t n -> p n t"),
+                    GELU,
+                )
+
+        h_codes = {}
+        h_scales = {}
+
+        def quantize_hidden(e):
+            h_codes[e] = tile([P, C], U32, "h_codes_%d" % e)
+            h_scales[e] = tile([P, C], U8, "h_scales_%d" % e)
+            nc.vector.quantize_mx(out=h_codes[e][:].bitcast(FP8X4), scales=h_scales[e][:], in_=hidden[e][:])
+
+        out_view = out.rearrange("(u p) c -> p u c", p=P)
+
+        def second_layer(e):
+            for pair in range(2):
+                bank = psum_y.tile([P, 2, C], F32, name="bank_y")
+                for i in range(2):
+                    cols = slice((2 * pair + i) * M, (2 * pair + i + 1) * M)
+                    nc.tensor.matmul_mx(
+                        out=bank[:, i, :],
+                        lhsT=codes["w2", e][:, cols].bitcast(FP8X4),
+                        lhsT_scale=scales["w2", e][:, cols],
+                        rhs=h_codes[e][:].bitcast(FP8X4),
+                        rhs_scale=h_scales[e][:],
+                        start=True,
+                        stop=True,
+                    )
+                y = tile([P, 2, C], F32, "y_%d_%d" % (e, pair))
+                if e == E - 1 and pair == 1:
+                    nc.vector.tensor_copy(y[:], bank[:])
+                else:
+                    nc.scalar.copy(y[:], bank[:])
+                nc.sync.dma_start(out_view[:, 2 * pair : 2 * pair + 2, e * C : (e + 1) * C], y[:])
+
+        gather_words(0)
+        gather_planes(0)
+        permute_wp(0)
+        gather_words(1)
+        cast("w1", 0, W1_SCALAR[0])
+        quantize("w1", 0)
+        first_layer(0)
+        gather_planes(1, "raw_w1_0")
+        permute_wp(1)
+        gather_words(2, "grouped_w1_0")
+        cast("w1", 1, W1_SCALAR[1])
+        quantize("w1", 1)
+        first_layer(1)
+        quantize_hidden(0)
+        cast("w2", 0, W2_SCALAR[0])
+        quantize("w2", 0)
+        second_layer(0)
+        gather_planes(2, "raw_w1_1")
+        permute_wp(2)
+        cast("w1", 2, W1_SCALAR[2])
+        quantize("w1", 2)
+        first_layer(2)
+        gather_words(3, "grouped_w1_1")
+        gather_planes(3, "raw_w2_0")
+        quantize_hidden(1)
+        cast("w2", 1, W2_SCALAR[1])
+        quantize("w2", 1)
+        second_layer(1)
+        permute_wp(3)
+        cast("w1", 3, W1_SCALAR[3])
+        quantize("w1", 3)
+        first_layer(3)
+        quantize_hidden(2)
+        cast("w2", 2, W2_SCALAR[2])
+        quantize("w2", 2)
+        second_layer(2)
+        quantize_hidden(3)
+        cast("w2", 3, W2_SCALAR[3])
+        quantize("w2", 3, 2)
+        second_layer(3)

@@ -1,6 +1,7 @@
 from contextlib import ExitStack
 
 import concourse.mybir as mybir
+from concourse.masks import make_identity
 
 K, T, E, C, H, N = 512, 512, 4, 256, 512, 512
 FLOPS = 2 * E * C * (2 * K * H + H * N)
@@ -19,10 +20,9 @@ P = 128
 PACK = 4
 M = 128
 ALIGN = 64
-LIST_COLS = C // 16
-
-W1_SCALAR = (512, 512, 512, 512)
-W2_SCALAR = (512, 0, 128, 192)
+WIDTH = 512
+WINDOW = 2 * T
+GROUP = 2 * C
 
 
 def tile_moe_duo_s_gelu_kernel(
@@ -32,138 +32,125 @@ def tile_moe_duo_s_gelu_kernel(
     with ExitStack() as ctx:
         lists = ctx.enter_context(tc.tile_pool(name="lists", bufs=1))
         sb = ctx.enter_context(tc.tile_pool(name="sb", bufs=1))
-        psum_h = ctx.enter_context(tc.psum_pool(name="psum_h", bufs=4))
-        psum_y = ctx.enter_context(tc.psum_pool(name="psum_y", bufs=4))
+        psum_h = ctx.enter_context(tc.psum_pool(name="psum_h", bufs=3))
+        psum_t = ctx.enter_context(tc.psum_pool(name="psum_t", bufs=2))
+        psum_y = ctx.enter_context(tc.psum_pool(name="psum_y", bufs=3))
 
         def tile(shape, dtype, name, tag=None):
             return sb.tile(shape, dtype, name=name, tag=tag or name, align_bytes=ALIGN)
 
-        token_list = lists.tile([P, E * LIST_COLS], U16, name="token_list")
-        partner_list = lists.tile([P, E * LIST_COLS], U16, name="partner_list")
-        x_codes = tile([P, T], I32, "x_codes")
-        x_plane = tile([P, T], U8, "x_plane")
-        wp_plane_raw = tile([P, E, H], U8, "wp_plane_raw")
+        token_list = lists.tile([P, E * C // 16], U16, name="token_list")
+        partner_list = lists.tile([P, E * C // 16], U16, name="partner_list")
+        x_codes = tile([P, WINDOW], I32, "x_codes")
+        x_plane = tile([P, WINDOW], U8, "x_plane")
+        wp_codes = tile([P, E, 2 * H], U8, "wp_codes")
+        wp_plane = tile([P, E, H], U8, "wp_plane")
+        identity = tile([P, P], F32, "identity")
+        warm = tile([P, 1], F32, "warm")
 
         nc.vector.memset(x_plane[:].bitcast(I32), 0)
-        nc.vector.memset(wp_plane_raw[:].bitcast(I32), 0)
+        nc.vector.memset(x_codes[:, T:], 0)
+        nc.vector.memset(wp_plane[:].bitcast(I32), 0)
+        make_identity(nc, identity[:])
+        nc.scalar.activation(warm[:], identity[:, 0:1], GELU)
 
-        nc.sync.dma_start(x_codes[:], x_words[0].rearrange("p t d -> p (t d)").bitcast(I32))
+        weights = {"w1": w1, "w2": w2}
+        halved = (("w1", 0), ("w1", 1), ("w2", E - 1))
+        raw = {}
+
+        def pieces(name, e):
+            return ((0, WIDTH // 2), (WIDTH // 2, WIDTH)) if (name, e) in halved else ((0, WIDTH),)
+
+        def load_matrix(name, e):
+            rows = weights[name][e].rearrange("(p j) c -> p j c", j=PACK)
+            for c0, c1 in pieces(name, e):
+                raw[name, e, c0] = tile([P, PACK, c1 - c0], F32, "raw_%s_%d_%d" % (name, e, c0))
+                nc.sync.dma_start(raw[name, e, c0][:], rows[:, :, c0:c1])
+
+        nc.sync.dma_start(x_codes[:, :T], x_words[0].rearrange("p t d -> p (t d)").bitcast(I32))
         nc.sync.dma_start(token_list[:], offs)
         nc.sync.dma_start(partner_list[:], offs2)
+        load_matrix("w1", 0)
         x_rows = x_scales[0].bitcast(I32).rearrange("(q r) c -> r q c", r=4)
         for r in range(4):
-            nc.sync.dma_start(x_plane[:].bitcast(I32)[r:P:32, :], x_rows[r])
-        wp_rows = wp_scales.bitcast(I32).rearrange("e s (q r) c -> r q (e s) c", r=4)
-
-        raw = {}
-        wp_raw = {}
-
-        def load_matrix(name, w, e):
-            raw[name, e] = tile([P, PACK, 512], F32, "raw_%s_%d" % (name, e))
-            nc.sync.dma_start(raw[name, e][:], w[e].rearrange("(p j) c -> p j c", j=PACK))
-
-        def load_wp(e):
-            wp_raw[e] = tile([P, 2 * H], U8, "wp_raw_%d" % e)
-            nc.sync.dma_start(wp_raw[e][:].bitcast(I32), wp_words[e, 0].bitcast(I32))
-
-        load_matrix("w1", w1, 0)
-        load_wp(0)
-        for r in range(4):
-            nc.sync.dma_start(wp_plane_raw[:].bitcast(I32)[r:P:32, :, :], wp_rows[r])
+            nc.sync.dma_start(x_plane[:].bitcast(I32)[r:P:32, : T // 4], x_rows[r])
         for e in range(1, E):
-            load_matrix("w1", w1, e)
-            load_wp(e)
-            load_matrix("w2", w2, e - 1)
-        load_matrix("w2", w2, E - 1)
+            load_matrix("w1", e)
+        nc.sync.dma_start(wp_codes[:].bitcast(I32), wp_words.bitcast(I32).rearrange("e s p c -> p (e s) c"))
+        wp_rows = wp_scales.bitcast(I32).rearrange("e s (q r) c -> r q (e s) c", r=4)
+        for r in range(4):
+            nc.sync.dma_start(wp_plane[:].bitcast(I32)[r:P:32, :, :], wp_rows[r])
+        for e in range(E):
+            load_matrix("w2", e)
 
         words = {}
         planes = {}
 
-        def gather_words(e, tag=None):
-            words[e] = tile([P, 2, C], U32, "words_%d" % e, tag)
+        def gather_words(g, tag=None):
+            words[g] = tile([P, 2, GROUP], U32, "words_%d" % g, tag)
             for s, lst in enumerate((token_list, partner_list)):
-                offsets = lst[:, e * LIST_COLS : (e + 1) * LIST_COLS]
-                nc.vector.tensor_copy(words[e][:, s, :], x_codes[:].bitcast(U32).indirect(offsets))
+                offsets = lst[:, g * GROUP // 16 : (g + 1) * GROUP // 16]
+                nc.vector.tensor_copy(words[g][:, s, :], x_codes[:].bitcast(U32).indirect(offsets))
 
-        def gather_planes(e, tag=None):
-            planes[e] = tile([P, 2, C], U8, "planes_%d" % e, tag)
+        def gather_planes(g, tag=None):
+            planes[g] = tile([P, 2, GROUP], U8, "planes_%d" % g, tag)
             for s, lst in enumerate((token_list, partner_list)):
-                offsets = lst[:, e * LIST_COLS : (e + 1) * LIST_COLS]
-                nc.vector.tensor_copy(planes[e][:, s, :], x_plane[:].indirect(offsets))
+                offsets = lst[:, g * GROUP // 16 : (g + 1) * GROUP // 16]
+                nc.vector.tensor_copy(planes[g][:, s, :], x_plane[:].indirect(offsets))
 
-        wp_codes = {}
-        wp_plane = {}
-
-        def permute_wp(e):
-            wp_codes[e] = tile([P, 2 * H], U8, "wp_codes_%d" % e)
-            wp_plane[e] = tile([P, H], U8, "wp_plane_%d" % e)
-            nc.vector.tensor_copy(
-                wp_codes[e][:].bitcast(U16).rearrange("p (t m) -> p m t", t=PACK),
-                wp_raw[e][:].bitcast(U16).rearrange("p (m t) -> p m t", t=PACK),
-            )
-            nc.vector.tensor_copy(
-                wp_plane[e][:].rearrange("p (t m) -> p t m", t=PACK),
-                wp_plane_raw[:, e, :].rearrange("p (m t) -> p t m", t=PACK),
-            )
-
-        grouped = {}
         codes = {}
         scales = {}
 
-        def cast(name, e, scalar_cols):
-            grouped[name, e] = tile([P, 512 * PACK], BF16, "grouped_%s_%d" % (name, e))
-            src = raw[name, e][:].rearrange("p j (m t) -> p m j t", t=4)
-            if name == "w1":
-                dst = grouped[name, e][:].rearrange("p (t m j) -> p m j t", t=4, j=PACK)
-            else:
-                dst = grouped[name, e][:].rearrange("p (m t j) -> p m j t", t=4, j=PACK)
-            cut = scalar_cols // 4
-            if cut > 0:
-                nc.scalar.copy(dst[:, :cut], src[:, :cut])
-            if cut < 128:
-                nc.vector.tensor_copy(dst[:, cut:], src[:, cut:])
+        def quantize_matrix(name, e):
+            codes[name, e] = tile([P, WIDTH], U32, "codes_%s_%d" % (name, e))
+            scales[name, e] = tile([P, WIDTH], U8, "scales_%s_%d" % (name, e))
+            for c0, c1 in pieces(name, e):
+                step = c1 - c0 if name == "w1" else (c1 - c0) // 2
+                grouped = {}
+                for a in range(c0, c1, step):
+                    grouped[a] = tile([P, step * PACK], BF16, "grouped_%s_%d_%d" % (name, e, a))
+                    src = raw[name, e, c0][:, :, a - c0 : a - c0 + step].rearrange("p j (m i) -> p m j i", i=4)
+                    dst = grouped[a][:].rearrange("p (m i j) -> p m j i", i=4, j=PACK)
+                    if name == "w1":
+                        nc.scalar.copy(dst, src)
+                    else:
+                        nc.vector.tensor_copy(dst, src)
+                for a in range(c0, c1, step):
+                    nc.vector.quantize_mx(
+                        out=codes[name, e][:, a : a + step].bitcast(FP8X4),
+                        scales=scales[name, e][:, a : a + step],
+                        in_=grouped[a][:],
+                    )
 
-        def quantize(name, e, pieces=1):
-            codes[name, e] = tile([P, 512], U32, "codes_%s_%d" % (name, e))
-            scales[name, e] = tile([P, 512], U8, "scales_%s_%d" % (name, e))
-            width = 512 // pieces
-            for i in range(pieces):
-                nc.vector.quantize_mx(
-                    out=codes[name, e][:, i * width : (i + 1) * width].bitcast(FP8X4),
-                    scales=scales[name, e][:, i * width : (i + 1) * width],
-                    in_=grouped[name, e][:, i * width * PACK : (i + 1) * width * PACK],
-                )
+        by_slot = {}
 
-        hidden = {}
-
-        def first_layer(e):
-            hidden[e] = tile([P, C * PACK], BF16, "hidden_%d" % e)
+        def first_layer(e, tag=None):
+            by_slot[e] = tile([P, 2 * H], BF16, "by_slot_%d" % e, tag)
             for half in range(C // M):
-                slots = slice(half * M, (half + 1) * M)
-                bank = psum_h.tile([P, PACK, M], F32, name="bank_h")
-                for t in range(PACK):
-                    cols = slice(t * M, (t + 1) * M)
-                    nc.tensor.matmul_mx(
-                        out=bank[:, t, :],
-                        lhsT=codes["w1", e][:, cols].bitcast(FP8X4),
-                        lhsT_scale=scales["w1", e][:, cols],
-                        rhs=words[e][:, 0, slots].bitcast(FP8X4),
-                        rhs_scale=planes[e][:, 0, slots],
-                        start=True,
-                        stop=False,
-                    )
-                    nc.tensor.matmul_mx(
-                        out=bank[:, t, :],
-                        lhsT=wp_codes[e][:, 2 * t * M : 2 * (t + 1) * M].bitcast(FP4X4),
-                        lhsT_scale=wp_plane[e][:, cols],
-                        rhs=words[e][:, 1, slots].bitcast(FP8X4),
-                        rhs_scale=planes[e][:, 1, slots],
-                        start=False,
-                        stop=True,
-                    )
+                first = (e % 2) * C + half * M
+                slots = slice(first, first + M)
+                bank = psum_h.tile([P, H], F32, name="bank_h")
+                nc.tensor.matmul_mx(
+                    out=bank[:],
+                    lhsT=words[e // 2][:, 0, slots].bitcast(FP8X4),
+                    lhsT_scale=planes[e // 2][:, 0, slots],
+                    rhs=codes["w1", e][:].bitcast(FP8X4),
+                    rhs_scale=scales["w1", e][:],
+                    start=True,
+                    stop=False,
+                )
+                nc.tensor.matmul_mx(
+                    out=bank[:],
+                    lhsT=words[e // 2][:, 1, slots].bitcast(FP8X4),
+                    lhsT_scale=planes[e // 2][:, 1, slots],
+                    rhs=wp_codes[:, e, :].bitcast(FP4X4),
+                    rhs_scale=wp_plane[:, e, :],
+                    start=False,
+                    stop=True,
+                )
                 nc.scalar.activation(
-                    hidden[e][:, half * M * PACK : (half + 1) * M * PACK].rearrange("p (n t) -> p n t", t=PACK),
-                    bank[:].rearrange("p t n -> p n t"),
+                    by_slot[e][:, half * H : (half + 1) * H].rearrange("s (u p d) -> s u p d", u=2, d=2),
+                    bank[:].rearrange("s (p u d) -> s u p d", u=2, d=2),
                     GELU,
                 )
 
@@ -171,9 +158,20 @@ def tile_moe_duo_s_gelu_kernel(
         h_scales = {}
 
         def quantize_hidden(e):
-            h_codes[e] = tile([P, C], U32, "h_codes_%d" % e)
+            bank = psum_t.tile([P, 2, 2, M], F32, name="bank_t")
+            pairs = by_slot[e][:].bitcast(F32)
+            for half in range(C // M):
+                for u in range(2):
+                    first = (2 * half + u) * P
+                    nc.tensor.transpose(bank[:, half, u, :], pairs[:, first : first + P], identity[:])
+            hidden = tile([P, C * PACK], BF16, "hidden_%d" % e)
+            nc.scalar.copy(
+                hidden[:].bitcast(F32).rearrange("p (h s u) -> p h s u", h=2, u=2),
+                bank[:].rearrange("p h u s -> p h s u"),
+            )
+            h_codes[e] = tile([P, C], U32, "h_codes_%d" % e, "raw_w2_%d_0" % e)
             h_scales[e] = tile([P, C], U8, "h_scales_%d" % e)
-            nc.vector.quantize_mx(out=h_codes[e][:].bitcast(FP8X4), scales=h_scales[e][:], in_=hidden[e][:])
+            nc.vector.quantize_mx(out=h_codes[e][:].bitcast(FP8X4), scales=h_scales[e][:], in_=hidden[:])
 
         out_view = out.rearrange("(u p) c -> p u c", p=P)
 
@@ -192,7 +190,7 @@ def tile_moe_duo_s_gelu_kernel(
                         stop=True,
                     )
                 y = tile([P, 2, C], F32, "y_%d_%d" % (e, pair))
-                if e == E - 1 and pair == 1:
+                if e == E - 1 and pair == 0:
                     nc.vector.tensor_copy(y[:], bank[:])
                 else:
                     nc.scalar.copy(y[:], bank[:])
@@ -200,41 +198,18 @@ def tile_moe_duo_s_gelu_kernel(
 
         gather_words(0)
         gather_planes(0)
-        permute_wp(0)
-        gather_words(1)
-        cast("w1", 0, W1_SCALAR[0])
-        quantize("w1", 0)
-        first_layer(0)
-        gather_planes(1, "raw_w1_0")
-        permute_wp(1)
-        gather_words(2, "grouped_w1_0")
-        cast("w1", 1, W1_SCALAR[1])
-        quantize("w1", 1)
-        first_layer(1)
-        quantize_hidden(0)
-        cast("w2", 0, W2_SCALAR[0])
-        quantize("w2", 0)
-        second_layer(0)
-        gather_planes(2, "raw_w1_1")
-        permute_wp(2)
-        cast("w1", 2, W1_SCALAR[2])
-        quantize("w1", 2)
-        first_layer(2)
-        gather_words(3, "grouped_w1_1")
-        gather_planes(3, "raw_w2_0")
-        quantize_hidden(1)
-        cast("w2", 1, W2_SCALAR[1])
-        quantize("w2", 1)
-        second_layer(1)
-        permute_wp(3)
-        cast("w1", 3, W1_SCALAR[3])
-        quantize("w1", 3)
-        first_layer(3)
-        quantize_hidden(2)
-        cast("w2", 2, W2_SCALAR[2])
-        quantize("w2", 2)
-        second_layer(2)
-        quantize_hidden(3)
-        cast("w2", 3, W2_SCALAR[3])
-        quantize("w2", 3, 2)
-        second_layer(3)
+        quantize_matrix("w1", 0)
+        gather_words(1, "grouped_w1_0_256")
+        quantize_matrix("w1", 1)
+        gather_planes(1, "grouped_w1_1_256")
+        quantize_matrix("w1", 2)
+        quantize_matrix("w1", 3)
+        first_layer(0, "raw_w1_3_0")
+        first_layer(1, "grouped_w1_3_0")
+        for e in range(E):
+            quantize_matrix("w2", e)
+            quantize_hidden(e)
+            if e + 2 < E:
+                first_layer(e + 2)
+        for e in range(E):
+            second_layer(e)

@@ -55,17 +55,11 @@ def tile_moe_duo_s_gelu_kernel(
         nc.scalar.activation(warm[:], identity[:, 0:1], GELU)
 
         weights = {"w1": w1, "w2": w2}
-        halved = (("w1", 0), ("w1", 1), ("w2", E - 1))
         raw = {}
 
-        def pieces(name, e):
-            return ((0, WIDTH // 2), (WIDTH // 2, WIDTH)) if (name, e) in halved else ((0, WIDTH),)
-
         def load_matrix(name, e):
-            rows = weights[name][e].rearrange("(p j) c -> p j c", j=PACK)
-            for c0, c1 in pieces(name, e):
-                raw[name, e, c0] = tile([P, PACK, c1 - c0], F32, "raw_%s_%d_%d" % (name, e, c0))
-                nc.sync.dma_start(raw[name, e, c0][:], rows[:, :, c0:c1])
+            raw[name, e] = tile([P, PACK, WIDTH], F32, "raw_%s_%d" % (name, e))
+            nc.sync.dma_start(raw[name, e][:], weights[name][e].rearrange("(p j) c -> p j c", j=PACK))
 
         nc.sync.dma_start(x_codes[:, :T], x_words[0].rearrange("p t d -> p (t d)").bitcast(I32))
         nc.sync.dma_start(token_list[:], offs)
@@ -101,26 +95,27 @@ def tile_moe_duo_s_gelu_kernel(
         codes = {}
         scales = {}
 
-        def quantize_matrix(name, e):
+        def quantize_matrix(name, e, copies):
             codes[name, e] = tile([P, WIDTH], U32, "codes_%s_%d" % (name, e))
             scales[name, e] = tile([P, WIDTH], U8, "scales_%s_%d" % (name, e))
-            for c0, c1 in pieces(name, e):
-                step = c1 - c0 if name == "w1" else (c1 - c0) // 2
-                grouped = {}
-                for a in range(c0, c1, step):
-                    grouped[a] = tile([P, step * PACK], BF16, "grouped_%s_%d_%d" % (name, e, a))
-                    src = raw[name, e, c0][:, :, a - c0 : a - c0 + step].rearrange("p j (m i) -> p m j i", i=4)
-                    dst = grouped[a][:].rearrange("p (m i j) -> p m j i", i=4, j=PACK)
-                    if name == "w1":
-                        nc.scalar.copy(dst, src)
-                    else:
-                        nc.vector.tensor_copy(dst, src)
-                for a in range(c0, c1, step):
-                    nc.vector.quantize_mx(
-                        out=codes[name, e][:, a : a + step].bitcast(FP8X4),
-                        scales=scales[name, e][:, a : a + step],
-                        in_=grouped[a][:],
-                    )
+            step = WIDTH // len(copies)
+            grouped = []
+
+            def quantize_part(i):
+                cols = slice(i * step, (i + 1) * step)
+                nc.vector.quantize_mx(
+                    out=codes[name, e][:, cols].bitcast(FP8X4), scales=scales[name, e][:, cols], in_=grouped[i][:]
+                )
+
+            for i, copy in enumerate(copies):
+                grouped.append(tile([P, step * PACK], BF16, "grouped_%s_%d_%d" % (name, e, i)))
+                copy(
+                    grouped[i][:].rearrange("p (m i j) -> p m j i", i=4, j=PACK),
+                    raw[name, e][:, :, i * step : (i + 1) * step].rearrange("p j (m i) -> p m j i", i=4),
+                )
+                if i > 0:
+                    quantize_part(i - 1)
+            quantize_part(len(copies) - 1)
 
         by_slot = {}
 
@@ -157,29 +152,30 @@ def tile_moe_duo_s_gelu_kernel(
         h_codes = {}
         h_scales = {}
 
-        def quantize_hidden(e):
+        def quantize_hidden(e, codes_tag, tag=None):
             bank = psum_t.tile([P, 2, 2, M], F32, name="bank_t")
             pairs = by_slot[e][:].bitcast(F32)
             for half in range(C // M):
                 for u in range(2):
                     first = (2 * half + u) * P
                     nc.tensor.transpose(bank[:, half, u, :], pairs[:, first : first + P], identity[:])
-            hidden = tile([P, C * PACK], BF16, "hidden_%d" % e)
+            hidden = tile([P, C * PACK], BF16, "hidden_%d" % e, tag)
             nc.scalar.copy(
                 hidden[:].bitcast(F32).rearrange("p (h s u) -> p h s u", h=2, u=2),
                 bank[:].rearrange("p h u s -> p h s u"),
             )
-            h_codes[e] = tile([P, C], U32, "h_codes_%d" % e, "raw_w2_%d_0" % e)
+            h_codes[e] = tile([P, C], U32, "h_codes_%d" % e, codes_tag)
             h_scales[e] = tile([P, C], U8, "h_scales_%d" % e)
             nc.vector.quantize_mx(out=h_codes[e][:].bitcast(FP8X4), scales=h_scales[e][:], in_=hidden[:])
 
         out_view = out.rearrange("(u p) c -> p u c", p=P)
 
-        def second_layer(e):
-            for pair in range(2):
-                bank = psum_y.tile([P, 2, C], F32, name="bank_y")
-                for i in range(2):
-                    cols = slice((2 * pair + i) * M, (2 * pair + i + 1) * M)
+        def second_layer(e, copies):
+            group = PACK // len(copies)
+            for g, copy in enumerate(copies):
+                bank = psum_y.tile([P, group, C], F32, name="bank_y")
+                for i in range(group):
+                    cols = slice((group * g + i) * M, (group * g + i + 1) * M)
                     nc.tensor.matmul_mx(
                         out=bank[:, i, :],
                         lhsT=codes["w2", e][:, cols].bitcast(FP8X4),
@@ -189,27 +185,31 @@ def tile_moe_duo_s_gelu_kernel(
                         start=True,
                         stop=True,
                     )
-                y = tile([P, 2, C], F32, "y_%d_%d" % (e, pair))
-                if e == E - 1 and pair == 0:
-                    nc.vector.tensor_copy(y[:], bank[:])
-                else:
-                    nc.scalar.copy(y[:], bank[:])
-                nc.sync.dma_start(out_view[:, 2 * pair : 2 * pair + 2, e * C : (e + 1) * C], y[:])
+                y = tile([P, group, C], F32, "y_%d_%d" % (e, g))
+                copy(y[:], bank[:])
+                nc.sync.dma_start(out_view[:, group * g : group * (g + 1), e * C : (e + 1) * C], y[:])
 
+        on_scalar, on_vector = nc.scalar.copy, nc.vector.tensor_copy
         gather_words(0)
+        gather_words(1)
         gather_planes(0)
-        quantize_matrix("w1", 0)
-        gather_words(1, "grouped_w1_0_256")
-        quantize_matrix("w1", 1)
-        gather_planes(1, "grouped_w1_1_256")
-        quantize_matrix("w1", 2)
-        quantize_matrix("w1", 3)
-        first_layer(0, "raw_w1_3_0")
-        first_layer(1, "grouped_w1_3_0")
-        for e in range(E):
-            quantize_matrix("w2", e)
-            quantize_hidden(e)
-            if e + 2 < E:
-                first_layer(e + 2)
-        for e in range(E):
-            second_layer(e)
+        quantize_matrix("w1", 0, [on_scalar])
+        gather_planes(1, "grouped_w1_0_0")
+        quantize_matrix("w1", 1, [on_scalar])
+        quantize_matrix("w1", 2, [on_scalar])
+        quantize_matrix("w1", 3, [on_vector, on_scalar])
+        first_layer(0, "raw_w1_3")
+        first_layer(1, "grouped_w1_3_1")
+        quantize_matrix("w2", 0, [on_vector] * 2)
+        quantize_hidden(0, "raw_w2_0")
+        quantize_matrix("w2", 1, [on_vector] * 2)
+        first_layer(2)
+        quantize_hidden(1, "raw_w2_1")
+        quantize_matrix("w2", 2, [on_vector] * 2)
+        first_layer(3)
+        quantize_hidden(2, "raw_w2_2")
+        quantize_hidden(3, "grouped_w2_2_1")
+        quantize_matrix("w2", 3, [on_vector] * 4)
+        for e in range(E - 1):
+            second_layer(e, [on_scalar] * 2)
+        second_layer(3, [on_scalar, on_scalar, on_vector, on_scalar])

@@ -68,12 +68,13 @@ def tile_moe_duo_s_gelu_kernel(
         x_rows = x_scales[0].bitcast(I32).rearrange("(q r) c -> r q c", r=4)
         for r in range(4):
             nc.sync.dma_start(x_plane[:].bitcast(I32)[r:P:32, : T // 4], x_rows[r])
-        for e in range(1, E):
+        for e in range(1, E - 1):
             load_matrix("w1", e)
         nc.sync.dma_start(wp_codes[:].bitcast(I32), wp_words.bitcast(I32).rearrange("e s p c -> p (e s) c"))
         wp_rows = wp_scales.bitcast(I32).rearrange("e s (q r) c -> r q (e s) c", r=4)
         for r in range(4):
             nc.sync.dma_start(wp_plane[:].bitcast(I32)[r:P:32, :, :], wp_rows[r])
+        load_matrix("w1", E - 1)
         for e in range(E):
             load_matrix("w2", e)
 
@@ -127,19 +128,19 @@ def tile_moe_duo_s_gelu_kernel(
                 bank = psum_h.tile([P, H], F32, name="bank_h")
                 nc.tensor.matmul_mx(
                     out=bank[:],
-                    lhsT=words[e // 2][:, 0, slots].bitcast(FP8X4),
-                    lhsT_scale=planes[e // 2][:, 0, slots],
-                    rhs=codes["w1", e][:].bitcast(FP8X4),
-                    rhs_scale=scales["w1", e][:],
+                    lhsT=words[e // 2][:, 1, slots].bitcast(FP8X4),
+                    lhsT_scale=planes[e // 2][:, 1, slots],
+                    rhs=wp_codes[:, e, :].bitcast(FP4X4),
+                    rhs_scale=wp_plane[:, e, :],
                     start=True,
                     stop=False,
                 )
                 nc.tensor.matmul_mx(
                     out=bank[:],
-                    lhsT=words[e // 2][:, 1, slots].bitcast(FP8X4),
-                    lhsT_scale=planes[e // 2][:, 1, slots],
-                    rhs=wp_codes[:, e, :].bitcast(FP4X4),
-                    rhs_scale=wp_plane[:, e, :],
+                    lhsT=words[e // 2][:, 0, slots].bitcast(FP8X4),
+                    lhsT_scale=planes[e // 2][:, 0, slots],
+                    rhs=codes["w1", e][:].bitcast(FP8X4),
+                    rhs_scale=scales["w1", e][:],
                     start=False,
                     stop=True,
                 )
@@ -197,16 +198,16 @@ def tile_moe_duo_s_gelu_kernel(
         gather_planes(1, "grouped_w1_0_0")
         quantize_matrix("w1", 1, [on_scalar])
         quantize_matrix("w1", 2, [on_scalar])
-        quantize_matrix("w1", 3, [on_vector, on_scalar])
-        first_layer(0, "raw_w1_3")
-        first_layer(1, "grouped_w1_3_1")
+        first_layer(0, "raw_w1_2")
+        first_layer(1, "grouped_w1_2_0")
+        quantize_matrix("w1", 3, [on_vector] * 2)
         quantize_matrix("w2", 0, [on_vector] * 2)
         quantize_hidden(0, "raw_w2_0")
-        quantize_matrix("w2", 1, [on_vector] * 2)
         first_layer(2)
+        quantize_matrix("w2", 1, [on_vector] * 2)
         quantize_hidden(1, "raw_w2_1")
-        quantize_matrix("w2", 2, [on_vector] * 2)
         first_layer(3)
+        quantize_matrix("w2", 2, [on_vector] * 2)
         quantize_hidden(2, "raw_w2_2")
         quantize_hidden(3, "grouped_w2_2_1")
         quantize_matrix("w2", 3, [on_vector] * 4)

@@ -74,8 +74,9 @@ def tile_moe_duo_s_gelu_kernel(
         wp_rows = wp_scales.bitcast(I32).rearrange("e s (q r) c -> r q (e s) c", r=4)
         for r in range(4):
             nc.sync.dma_start(wp_plane[:].bitcast(I32)[r:P:32, :, :], wp_rows[r])
+        load_matrix("w2", 0)
         load_matrix("w1", E - 1)
-        for e in range(E):
+        for e in range(1, E):
             load_matrix("w2", e)
 
         words = {}
@@ -153,21 +154,25 @@ def tile_moe_duo_s_gelu_kernel(
         h_codes = {}
         h_scales = {}
 
-        def quantize_hidden(e, codes_tag, tag=None):
+        hidden = {}
+
+        def turn_hidden(e):
             bank = psum_t.tile([P, 2, 2, M], F32, name="bank_t")
             pairs = by_slot[e][:].bitcast(F32)
             for half in range(C // M):
                 for u in range(2):
                     first = (2 * half + u) * P
                     nc.tensor.transpose(bank[:, half, u, :], pairs[:, first : first + P], identity[:])
-            hidden = tile([P, C * PACK], BF16, "hidden_%d" % e, tag)
+            hidden[e] = tile([P, C * PACK], BF16, "hidden_%d" % e)
             nc.scalar.copy(
-                hidden[:].bitcast(F32).rearrange("p (h s u) -> p h s u", h=2, u=2),
+                hidden[e][:].bitcast(F32).rearrange("p (h s u) -> p h s u", h=2, u=2),
                 bank[:].rearrange("p h u s -> p h s u"),
             )
+
+        def quantize_hidden(e, codes_tag):
             h_codes[e] = tile([P, C], U32, "h_codes_%d" % e, codes_tag)
             h_scales[e] = tile([P, C], U8, "h_scales_%d" % e)
-            nc.vector.quantize_mx(out=h_codes[e][:].bitcast(FP8X4), scales=h_scales[e][:], in_=hidden[:])
+            nc.vector.quantize_mx(out=h_codes[e][:].bitcast(FP8X4), scales=h_scales[e][:], in_=hidden[e][:])
 
         out_view = out.rearrange("(u p) c -> p u c", p=P)
 
@@ -198,19 +203,24 @@ def tile_moe_duo_s_gelu_kernel(
         gather_planes(1, "grouped_w1_0_0")
         quantize_matrix("w1", 1, [on_scalar])
         quantize_matrix("w1", 2, [on_scalar])
-        first_layer(0, "raw_w1_2")
-        first_layer(1, "grouped_w1_2_0")
-        quantize_matrix("w1", 3, [on_vector] * 2)
+        first_layer(0)
+        first_layer(1)
+        turn_hidden(0)
         quantize_matrix("w2", 0, [on_vector] * 2)
-        quantize_hidden(0, "raw_w2_0")
         first_layer(2)
+        turn_hidden(1)
+        quantize_matrix("w1", 3, [on_vector] * 2)
+        quantize_hidden(0, "raw_w1_3")
+        turn_hidden(2)
+        second_layer(0, [on_scalar] * 2)
+        first_layer(3)
         quantize_matrix("w2", 1, [on_vector] * 2)
         quantize_hidden(1, "raw_w2_1")
-        first_layer(3)
+        turn_hidden(3)
         quantize_matrix("w2", 2, [on_vector] * 2)
         quantize_hidden(2, "raw_w2_2")
         quantize_hidden(3, "grouped_w2_2_1")
+        second_layer(1, [on_scalar] * 2)
         quantize_matrix("w2", 3, [on_vector] * 4)
-        for e in range(E - 1):
-            second_layer(e, [on_scalar] * 2)
+        second_layer(2, [on_scalar] * 2)
         second_layer(3, [on_scalar, on_scalar, on_vector, on_scalar])

@@ -46,13 +46,11 @@ def tile_moe_duo_s_gelu_kernel(
         wp_codes = tile([P, E, 2 * H], U8, "wp_codes")
         wp_plane = tile([P, E, H], U8, "wp_plane")
         identity = tile([P, P], F32, "identity")
-        warm = tile([P, 1], F32, "warm")
 
         nc.vector.memset(x_plane[:].bitcast(I32), 0)
         nc.vector.memset(x_codes[:, T:], 0)
         nc.vector.memset(wp_plane[:].bitcast(I32), 0)
         make_identity(nc, identity[:])
-        nc.scalar.activation(warm[:], identity[:, 0:1], GELU)
 
         weights = {"w1": w1, "w2": w2}
         raw = {}

@@ -32,9 +32,7 @@ def tile_moe_duo_s_gelu_kernel(
     with ExitStack() as ctx:
         lists = ctx.enter_context(tc.tile_pool(name="lists", bufs=1))
         sb = ctx.enter_context(tc.tile_pool(name="sb", bufs=1))
-        psum_h = ctx.enter_context(tc.psum_pool(name="psum_h", bufs=3))
-        psum_t = ctx.enter_context(tc.psum_pool(name="psum_t", bufs=2))
-        psum_y = ctx.enter_context(tc.psum_pool(name="psum_y", bufs=3))
+        psum = ctx.enter_context(tc.psum_pool(name="psum", bufs=1))
 
         def tile(shape, dtype, name, tag=None):
             return sb.tile(shape, dtype, name=name, tag=tag or name, align_bytes=ALIGN)
@@ -48,6 +46,9 @@ def tile_moe_duo_s_gelu_kernel(
         identity = tile([P, P], F32, "identity")
 
         nc.vector.memset(x_plane[:].bitcast(I32), 0)
+        warm = tile([P, 16], F32, "warm")
+        nc.vector.memset(warm[:, :8], 0)
+        nc.scalar.activation(warm[:, 8:], warm[:, :8], GELU)
         nc.vector.memset(x_codes[:, T:], 0)
         nc.vector.memset(wp_plane[:].bitcast(I32), 0)
         make_identity(nc, identity[:])
@@ -95,54 +96,58 @@ def tile_moe_duo_s_gelu_kernel(
         codes = {}
         scales = {}
 
-        def quantize_matrix(name, e, copies):
-            codes[name, e] = tile([P, WIDTH], U32, "codes_%s_%d" % (name, e))
-            scales[name, e] = tile([P, WIDTH], U8, "scales_%s_%d" % (name, e))
-            step = WIDTH // len(copies)
-            grouped = []
+        grouped = {}
 
-            def quantize_part(i):
-                cols = slice(i * step, (i + 1) * step)
-                nc.vector.quantize_mx(
-                    out=codes[name, e][:, cols].bitcast(FP8X4), scales=scales[name, e][:, cols], in_=grouped[i][:]
-                )
+        def round_part(name, e, part, first, width, copy):
+            if (name, e, part) not in grouped:
+                grouped[name, e, part] = tile([P, (part[1] - part[0]) * PACK], BF16, "grouped_%s_%d_%d" % (name, e, part[0]))
+            at = (first - part[0]) * PACK
+            copy(
+                grouped[name, e, part][:, at : at + width * PACK].rearrange("p (m i j) -> p m j i", i=4, j=PACK),
+                raw[name, e][:, :, first : first + width].rearrange("p j (m i) -> p m j i", i=4),
+            )
 
-            for i, copy in enumerate(copies):
-                grouped.append(tile([P, step * PACK], BF16, "grouped_%s_%d_%d" % (name, e, i)))
-                copy(
-                    grouped[i][:].rearrange("p (m i j) -> p m j i", i=4, j=PACK),
-                    raw[name, e][:, :, i * step : (i + 1) * step].rearrange("p j (m i) -> p m j i", i=4),
-                )
-                if i > 0:
-                    quantize_part(i - 1)
-            quantize_part(len(copies) - 1)
+        def quantize_part(name, e, part):
+            if (name, e) not in codes:
+                codes[name, e] = tile([P, WIDTH], U32, "codes_%s_%d" % (name, e))
+                scales[name, e] = tile([P, WIDTH], U8, "scales_%s_%d" % (name, e))
+            cols = slice(part[0], part[1])
+            nc.vector.quantize_mx(
+                out=codes[name, e][:, cols].bitcast(FP8X4), scales=scales[name, e][:, cols], in_=grouped[name, e, part][:]
+            )
+
+        def scalar_matrix(name, e):
+            round_part(name, e, (0, WIDTH), 0, WIDTH, nc.scalar.copy)
+            quantize_part(name, e, (0, WIDTH))
+
+        def vector_matrix(name, e, parts):
+            for part in parts:
+                round_part(name, e, part, part[0], part[1] - part[0], nc.vector.tensor_copy)
+            for part in parts:
+                quantize_part(name, e, part)
 
         by_slot = {}
 
-        def first_layer(e, tag=None):
+        def first_layer(e, sides, banks, tag=None):
             by_slot[e] = tile([P, 2 * H], BF16, "by_slot_%d" % e, tag)
+            moving = (
+                (codes["w1", e][:].bitcast(FP8X4), scales["w1", e][:]),
+                (wp_codes[:, e, :].bitcast(FP4X4), wp_plane[:, e, :]),
+            )
             for half in range(C // M):
                 first = (e % 2) * C + half * M
                 slots = slice(first, first + M)
-                bank = psum_h.tile([P, H], F32, name="bank_h")
-                nc.tensor.matmul_mx(
-                    out=bank[:],
-                    lhsT=words[e // 2][:, 1, slots].bitcast(FP8X4),
-                    lhsT_scale=planes[e // 2][:, 1, slots],
-                    rhs=wp_codes[:, e, :].bitcast(FP4X4),
-                    rhs_scale=wp_plane[:, e, :],
-                    start=True,
-                    stop=False,
-                )
-                nc.tensor.matmul_mx(
-                    out=bank[:],
-                    lhsT=words[e // 2][:, 0, slots].bitcast(FP8X4),
-                    lhsT_scale=planes[e // 2][:, 0, slots],
-                    rhs=codes["w1", e][:].bitcast(FP8X4),
-                    rhs_scale=scales["w1", e][:],
-                    start=False,
-                    stop=True,
-                )
+                bank = psum.tile([P, H], F32, name="bank", tag="bank_%d" % banks[half])
+                for side in sides:
+                    nc.tensor.matmul_mx(
+                        out=bank[:],
+                        lhsT=words[e // 2][:, side, slots].bitcast(FP8X4),
+                        lhsT_scale=planes[e // 2][:, side, slots],
+                        rhs=moving[side][0],
+                        rhs_scale=moving[side][1],
+                        start=side == sides[0],
+                        stop=side == sides[1],
+                    )
                 nc.scalar.activation(
                     by_slot[e][:, half * H : (half + 1) * H].rearrange("s (u p d) -> s u p d", u=2, d=2),
                     bank[:].rearrange("s (p u d) -> s u p d", u=2, d=2),
@@ -154,14 +159,14 @@ def tile_moe_duo_s_gelu_kernel(
 
         hidden = {}
 
-        def turn_hidden(e):
-            bank = psum_t.tile([P, 2, 2, M], F32, name="bank_t")
+        def turn_hidden(e, number, tag=None):
+            bank = psum.tile([P, 2, 2, M], F32, name="bank", tag="bank_%d" % number)
             pairs = by_slot[e][:].bitcast(F32)
             for half in range(C // M):
                 for u in range(2):
                     first = (2 * half + u) * P
                     nc.tensor.transpose(bank[:, half, u, :], pairs[:, first : first + P], identity[:])
-            hidden[e] = tile([P, C * PACK], BF16, "hidden_%d" % e)
+            hidden[e] = tile([P, C * PACK], BF16, "hidden_%d" % e, tag)
             nc.scalar.copy(
                 hidden[e][:].bitcast(F32).rearrange("p (h s u) -> p h s u", h=2, u=2),
                 bank[:].rearrange("p h u s -> p h s u"),
@@ -174,51 +179,92 @@ def tile_moe_duo_s_gelu_kernel(
 
         out_view = out.rearrange("(u p) c -> p u c", p=P)
 
-        def second_layer(e, copies):
-            group = PACK // len(copies)
-            for g, copy in enumerate(copies):
-                bank = psum_y.tile([P, group, C], F32, name="bank_y")
-                for i in range(group):
-                    cols = slice((group * g + i) * M, (group * g + i + 1) * M)
-                    nc.tensor.matmul_mx(
-                        out=bank[:, i, :],
-                        lhsT=codes["w2", e][:, cols].bitcast(FP8X4),
-                        lhsT_scale=scales["w2", e][:, cols],
-                        rhs=h_codes[e][:].bitcast(FP8X4),
-                        rhs_scale=h_scales[e][:],
-                        start=True,
-                        stop=True,
-                    )
-                y = tile([P, group, C], F32, "y_%d_%d" % (e, g))
-                copy(y[:], bank[:])
-                nc.sync.dma_start(out_view[:, group * g : group * (g + 1), e * C : (e + 1) * C], y[:])
+        staged = {}
+
+        def stage(first, count, first_expert, experts, tag=None):
+            rows = tile([P, count, experts * C], F32, "staged_%d_%d" % (first, first_expert), tag)
+            for u in range(first, first + count):
+                for e in range(first_expert, first_expert + experts):
+                    staged[u, e] = (rows, first, first_expert)
+
+        def second_layer(e, first, count, number, copy):
+            bank = psum.tile([P, count, C], F32, name="bank", tag="bank_%d" % number)
+            for i in range(count):
+                cols = slice((first + i) * M, (first + i + 1) * M)
+                nc.tensor.matmul_mx(
+                    out=bank[:, i, :],
+                    lhsT=codes["w2", e][:, cols].bitcast(FP8X4),
+                    lhsT_scale=scales["w2", e][:, cols],
+                    rhs=h_codes[e][:].bitcast(FP8X4),
+                    rhs_scale=h_scales[e][:],
+                    start=True,
+                    stop=True,
+                )
+            rows, row_0, expert_0 = staged[first, e]
+            at = (e - expert_0) * C
+            copy(rows[:, first - row_0 : first - row_0 + count, at : at + C], bank[:])
+
+        def store(first, e):
+            rows, row_0, expert_0 = staged[first, e]
+            count, width = rows.shape[1], rows.shape[2]
+            nc.sync.dma_start(out_view[:, row_0 : row_0 + count, expert_0 * C : expert_0 * C + width], rows[:])
 
         on_scalar, on_vector = nc.scalar.copy, nc.vector.tensor_copy
+        token_first, partner_first = (0, 1), (1, 0)
+        low, high = (0, 2 * M), (2 * M, 4 * M)
+        quarters = [(u * M, (u + 1) * M) for u in range(PACK)]
         gather_words(0)
         gather_words(1)
         gather_planes(0)
-        quantize_matrix("w1", 0, [on_scalar])
-        gather_planes(1, "grouped_w1_0_0")
-        quantize_matrix("w1", 1, [on_scalar])
-        quantize_matrix("w1", 2, [on_scalar])
-        first_layer(0)
-        first_layer(1)
-        turn_hidden(0)
-        quantize_matrix("w2", 0, [on_vector] * 2)
-        first_layer(2)
-        turn_hidden(1)
-        quantize_matrix("w1", 3, [on_vector] * 2)
-        quantize_hidden(0, "raw_w1_3")
-        turn_hidden(2)
-        second_layer(0, [on_scalar] * 2)
-        first_layer(3)
-        quantize_matrix("w2", 1, [on_vector] * 2)
-        quantize_hidden(1, "raw_w2_1")
-        turn_hidden(3)
-        quantize_matrix("w2", 2, [on_vector] * 2)
-        quantize_hidden(2, "raw_w2_2")
-        quantize_hidden(3, "grouped_w2_2_1")
-        second_layer(1, [on_scalar] * 2)
-        quantize_matrix("w2", 3, [on_vector] * 4)
-        second_layer(2, [on_scalar] * 2)
-        second_layer(3, [on_scalar, on_scalar, on_vector, on_scalar])
+        scalar_matrix("w1", 0)
+        scalar_matrix("w1", 1)
+        gather_planes(1, "grouped_w1_1_0")
+        scalar_matrix("w1", 2)
+        first_layer(0, token_first, (0, 1))
+        first_layer(1, partner_first, (2, 5))
+        turn_hidden(0, 3)
+        vector_matrix("w2", 0, (low, high))
+        quantize_hidden(0, "raw_w2_0")
+        first_layer(2, partner_first, (0, 1))
+        turn_hidden(1, 4)
+        vector_matrix("w1", 3, (low, high))
+        quantize_hidden(1, "raw_w1_3")
+        turn_hidden(2, 3)
+        stage(0, 4, 0, 1)
+        second_layer(0, 0, 2, 6, on_scalar)
+        second_layer(0, 2, 2, 7, on_scalar)
+        store(0, 0)
+        first_layer(3, partner_first, (2, 5))
+        vector_matrix("w2", 1, (low, high))
+        quantize_hidden(2, "raw_w2_1")
+        stage(0, 2, 1, 1)
+        stage(2, 2, 1, 1)
+        second_layer(1, 0, 2, 0, on_scalar)
+        store(0, 1)
+        second_layer(1, 2, 2, 1, on_scalar)
+        store(2, 1)
+        turn_hidden(3, 0)
+        vector_matrix("w2", 2, (low, high))
+        stage(0, 2, 2, 1)
+        stage(2, 2, 2, 1)
+        second_layer(2, 0, 2, 6, on_scalar)
+        store(0, 2)
+        second_layer(2, 2, 2, 7, on_scalar)
+        store(2, 2)
+        for u in range(PACK):
+            round_part("w2", 3, quarters[u], u * M, M, on_vector)
+            if u > 0:
+                quantize_part("w2", 3, quarters[u - 1])
+            if u == 1:
+                quantize_hidden(3, "grouped_w2_3_0")
+        quantize_part("w2", 3, quarters[3])
+        stage(0, 2, 3, 1)
+        stage(2, 1, 3, 1)
+        stage(3, 1, 3, 1)
+        second_layer(3, 0, 1, 2, on_scalar)
+        second_layer(3, 1, 1, 5, on_scalar)
+        store(0, 3)
+        second_layer(3, 2, 1, 3, on_vector)
+        store(2, 3)
+        second_layer(3, 3, 1, 4, on_scalar)
+        store(3, 3)

@@ -103,8 +103,8 @@ def tile_moe_duo_s_gelu_kernel(
                 grouped[name, e, part] = tile([P, (part[1] - part[0]) * PACK], BF16, "grouped_%s_%d_%d" % (name, e, part[0]))
             at = (first - part[0]) * PACK
             copy(
-                grouped[name, e, part][:, at : at + width * PACK].rearrange("p (m i j) -> p m j i", i=4, j=PACK),
-                raw[name, e][:, :, first : first + width].rearrange("p j (m i) -> p m j i", i=4),
+                grouped[name, e, part][:, at : at + width * PACK].rearrange("p (m i u d) -> p m u i d", i=4, u=2, d=2),
+                raw[name, e][:, :, first : first + width].rearrange("p (u d) (m i) -> p m u i d", i=4, d=2),
             )
 
         def quantize_part(name, e, part):

@@ -41,7 +41,8 @@ def tile_moe_duo_s_gelu_kernel(
         partner_list = lists.tile([P, E * C // 16], U16, name="partner_list")
         x_codes = tile([P, WINDOW], I32, "x_codes")
         x_plane = tile([P, WINDOW], U8, "x_plane")
-        wp_codes = tile([P, E, 2 * H], U8, "wp_codes")
+        wp_pair = [tile([P, 2, 2 * H], U8, "wp_pair_%d" % g) for g in range(2)]
+        wp_codes = [wp_pair[e // 2][:, e % 2, :] for e in range(E)]
         wp_plane = tile([P, E, H], U8, "wp_plane")
         identity = tile([P, P], F32, "identity")
 
@@ -69,14 +70,20 @@ def tile_moe_duo_s_gelu_kernel(
             nc.sync.dma_start(x_plane[:].bitcast(I32)[r:P:32, : T // 4], x_rows[r])
         for e in range(1, E - 1):
             load_matrix("w1", e)
-        nc.sync.dma_start(wp_codes[:].bitcast(I32), wp_words.bitcast(I32).rearrange("e s p c -> p (e s) c"))
+        wp_by_partition = wp_words.bitcast(I32).rearrange("e s p c -> p (e s) c")
+        nc.sync.dma_start(wp_pair[0][:].bitcast(I32), wp_by_partition[:, :2, :])
         wp_rows = wp_scales.bitcast(I32).rearrange("e s (q r) c -> r q (e s) c", r=4)
         for r in range(4):
             nc.sync.dma_start(wp_plane[:].bitcast(I32)[r:P:32, :, :], wp_rows[r])
         load_matrix("w2", 0)
+        nc.sync.dma_start(wp_pair[1][:].bitcast(I32), wp_by_partition[:, 2:, :])
         load_matrix("w1", E - 1)
-        for e in range(1, E):
+        for e in range(1, E - 1):
             load_matrix("w2", e)
+        last = w2[E - 1].rearrange("(p j) c -> p j c", j=PACK)
+        last_half = [tile([P, PACK, WIDTH // 2], F32, "last_half_%d" % h) for h in range(2)]
+        for h in range(2):
+            nc.sync.dma_start(last_half[h][:], last[:, :, h * WIDTH // 2 : (h + 1) * WIDTH // 2])
 
         words = {}
         planes = {}
@@ -102,9 +109,14 @@ def tile_moe_duo_s_gelu_kernel(
             if (name, e, part) not in grouped:
                 grouped[name, e, part] = tile([P, (part[1] - part[0]) * PACK], BF16, "grouped_%s_%d_%d" % (name, e, part[0]))
             at = (first - part[0]) * PACK
+            if (name, e) in raw:
+                source = raw[name, e][:, :, first : first + width]
+            else:
+                inside = first % (WIDTH // 2)
+                source = last_half[first // (WIDTH // 2)][:, :, inside : inside + width]
             copy(
                 grouped[name, e, part][:, at : at + width * PACK].rearrange("p (m i u d) -> p m u i d", i=4, u=2, d=2),
-                raw[name, e][:, :, first : first + width].rearrange("p (u d) (m i) -> p m u i d", i=4, d=2),
+                source.rearrange("p (u d) (m i) -> p m u i d", i=4, d=2),
             )
 
         def quantize_part(name, e, part):
@@ -132,7 +144,7 @@ def tile_moe_duo_s_gelu_kernel(
             by_slot[e] = tile([P, 2 * H], BF16, "by_slot_%d" % e, tag)
             moving = (
                 (codes["w1", e][:].bitcast(FP8X4), scales["w1", e][:]),
-                (wp_codes[:, e, :].bitcast(FP4X4), wp_plane[:, e, :]),
+                (wp_codes[e].bitcast(FP4X4), wp_plane[:, e, :]),
             )
             for half in range(C // M):
                 first = (e % 2) * C + half * M

@@ -78,12 +78,8 @@ def tile_moe_duo_s_gelu_kernel(
         load_matrix("w2", 0)
         nc.sync.dma_start(wp_pair[1][:].bitcast(I32), wp_by_partition[:, 2:, :])
         load_matrix("w1", E - 1)
-        for e in range(1, E - 1):
+        for e in range(1, E):
             load_matrix("w2", e)
-        last = w2[E - 1].rearrange("(p j) c -> p j c", j=PACK)
-        last_half = [tile([P, PACK, WIDTH // 2], F32, "last_half_%d" % h) for h in range(2)]
-        for h in range(2):
-            nc.sync.dma_start(last_half[h][:], last[:, :, h * WIDTH // 2 : (h + 1) * WIDTH // 2])
 
         words = {}
         planes = {}
@@ -109,11 +105,7 @@ def tile_moe_duo_s_gelu_kernel(
             if (name, e, part) not in grouped:
                 grouped[name, e, part] = tile([P, (part[1] - part[0]) * PACK], BF16, "grouped_%s_%d_%d" % (name, e, part[0]))
             at = (first - part[0]) * PACK
-            if (name, e) in raw:
-                source = raw[name, e][:, :, first : first + width]
-            else:
-                inside = first % (WIDTH // 2)
-                source = last_half[first // (WIDTH // 2)][:, :, inside : inside + width]
+            source = raw[name, e][:, :, first : first + width]
             copy(
                 grouped[name, e, part][:, at : at + width * PACK].rearrange("p (m i u d) -> p m u i d", i=4, u=2, d=2),
                 source.rearrange("p (u d) (m i) -> p m u i d", i=4, d=2),

@@ -22,7 +22,9 @@ M = 128
 ALIGN = 64
 WIDTH = 512
 WINDOW = 2 * T
+WORD_WINDOW = 1408
 GROUP = 2 * C
+SHARE = 64
 
 
 def tile_moe_duo_s_gelu_kernel(
@@ -39,7 +41,7 @@ def tile_moe_duo_s_gelu_kernel(
 
         token_list = lists.tile([P, E * C // 16], U16, name="token_list")
         partner_list = lists.tile([P, E * C // 16], U16, name="partner_list")
-        x_codes = tile([P, WINDOW], I32, "x_codes")
+        x_codes = tile([P, WORD_WINDOW], I32, "x_codes")
         x_plane = tile([P, WINDOW], U8, "x_plane")
         wp_pair = [tile([P, 2, 2 * H], U8, "wp_pair_%d" % g) for g in range(2)]
         wp_codes = [wp_pair[e // 2][:, e % 2, :] for e in range(E)]
@@ -84,11 +86,10 @@ def tile_moe_duo_s_gelu_kernel(
         words = {}
         planes = {}
 
-        def gather_words(g, tag=None):
-            words[g] = tile([P, 2, GROUP], U32, "words_%d" % g, tag)
+        def gather_words():
             for s, lst in enumerate((token_list, partner_list)):
-                offsets = lst[:, g * GROUP // 16 : (g + 1) * GROUP // 16]
-                nc.vector.tensor_copy(words[g][:, s, :], x_codes[:].bitcast(U32).indirect(offsets))
+                words[s] = tile([P, E * C], U32, "words_%d" % s)
+                nc.vector.tensor_copy(words[s][:], x_codes[:].bitcast(U32).indirect(lst[:]))
 
         def gather_planes(g, tag=None):
             planes[g] = tile([P, 2, GROUP], U8, "planes_%d" % g, tag)
@@ -145,7 +146,7 @@ def tile_moe_duo_s_gelu_kernel(
                 for side in sides:
                     nc.tensor.matmul_mx(
                         out=bank[:],
-                        lhsT=words[e // 2][:, side, slots].bitcast(FP8X4),
+                        lhsT=words[side][:, e * C + half * M : e * C + (half + 1) * M].bitcast(FP8X4),
                         lhsT_scale=planes[e // 2][:, side, slots],
                         rhs=moving[side][0],
                         rhs_scale=moving[side][1],
@@ -217,13 +218,14 @@ def tile_moe_duo_s_gelu_kernel(
         token_first, partner_first = (0, 1), (1, 0)
         low, high = (0, 2 * M), (2 * M, 4 * M)
         quarters = [(u * M, (u + 1) * M) for u in range(PACK)]
-        gather_words(0)
-        gather_words(1)
+        gather_words()
         gather_planes(0)
         scalar_matrix("w1", 0)
         scalar_matrix("w1", 1)
         gather_planes(1, "grouped_w1_1_0")
-        scalar_matrix("w1", 2)
+        round_part("w1", 2, (0, WIDTH), SHARE, WIDTH - SHARE, on_scalar)
+        round_part("w1", 2, (0, WIDTH), 0, SHARE, on_vector)
+        quantize_part("w1", 2, (0, WIDTH))
         first_layer(0, token_first, (0, 1))
         first_layer(1, partner_first, (2, 5))
         turn_hidden(0, 3)

@@ -264,12 +264,14 @@ def tile_moe_duo_s_gelu_kernel(
             if u == 1:
                 quantize_hidden(3, "grouped_w2_3_0")
         quantize_part("w2", 3, quarters[3])
-        stage(0, 2, 3, 1)
+        stage(0, 1, 3, 1)
+        stage(1, 1, 3, 1)
         stage(2, 1, 3, 1)
         stage(3, 1, 3, 1)
         second_layer(3, 0, 1, 2, on_scalar)
-        second_layer(3, 1, 1, 5, on_scalar)
         store(0, 3)
+        second_layer(3, 1, 1, 5, on_scalar)
+        store(1, 3)
         second_layer(3, 2, 1, 3, on_vector)
         store(2, 3)
         second_layer(3, 3, 1, 4, on_scalar)

@@ -24,7 +24,6 @@ WIDTH = 512
 WINDOW = 2 * T
 WORD_WINDOW = 1408
 GROUP = 2 * C
-SHARE = 64
 
 
 def tile_moe_duo_s_gelu_kernel(
@@ -34,9 +33,14 @@ def tile_moe_duo_s_gelu_kernel(
     with ExitStack() as ctx:
         lists = ctx.enter_context(tc.tile_pool(name="lists", bufs=1))
         sb = ctx.enter_context(tc.tile_pool(name="sb", bufs=1))
+        held = ctx.enter_context(tc.tile_pool(name="held", bufs=1))
         psum = ctx.enter_context(tc.psum_pool(name="psum", bufs=1))
 
+        placed = {"grouped_w1_1_0": 0, "planes_1": 0, "grouped_w1_2_256": 2 * GROUP}
+
         def tile(shape, dtype, name, tag=None):
+            if name in placed:
+                return held.tile(shape, dtype, name=name, align_bytes=ALIGN, offset=placed[name])
             return sb.tile(shape, dtype, name=name, tag=tag or name, align_bytes=ALIGN)
 
         token_list = lists.tile([P, E * C // 16], U16, name="token_list")
@@ -53,7 +57,10 @@ def tile_moe_duo_s_gelu_kernel(
         nc.vector.memset(warm[:, :8], 0)
         nc.scalar.activation(warm[:, 8:], warm[:, :8], GELU)
         nc.vector.memset(x_codes[:, T:], 0)
-        nc.vector.memset(wp_plane[:].bitcast(I32), 0)
+        nc.gpsimd.memset(wp_plane[:].bitcast(I32), 0)
+        wp_rows = wp_scales.bitcast(I32).rearrange("e s (q r) c -> r q (e s) c", r=4)
+        for r in range(4):
+            nc.gpsimd.dma_start(wp_plane[:].bitcast(I32)[r:P:32, :, :], wp_rows[r])
         make_identity(nc, identity[:])
 
         weights = {"w1": w1, "w2": w2}
@@ -74,9 +81,6 @@ def tile_moe_duo_s_gelu_kernel(
             load_matrix("w1", e)
         wp_by_partition = wp_words.bitcast(I32).rearrange("e s p c -> p (e s) c")
         nc.sync.dma_start(wp_pair[0][:].bitcast(I32), wp_by_partition[:, :2, :])
-        wp_rows = wp_scales.bitcast(I32).rearrange("e s (q r) c -> r q (e s) c", r=4)
-        for r in range(4):
-            nc.sync.dma_start(wp_plane[:].bitcast(I32)[r:P:32, :, :], wp_rows[r])
         load_matrix("w2", 0)
         nc.sync.dma_start(wp_pair[1][:].bitcast(I32), wp_by_partition[:, 2:, :])
         load_matrix("w1", E - 1)
@@ -110,6 +114,17 @@ def tile_moe_duo_s_gelu_kernel(
             copy(
                 grouped[name, e, part][:, at : at + width * PACK].rearrange("p (m i u d) -> p m u i d", i=4, u=2, d=2),
                 source.rearrange("p (u d) (m i) -> p m u i d", i=4, d=2),
+            )
+
+        def round_on_gpsimd(name, e, part):
+            grouped[name, e, part] = tile([P, (part[1] - part[0]) * PACK], BF16, "grouped_%s_%d_%d" % (name, e, part[0]))
+            nc.gpsimd.tensor_scalar(
+                grouped[name, e, part][:].rearrange("p (c j) -> p c j", j=PACK),
+                raw[name, e][:, :, part[0] : part[1]].rearrange("p j c -> p c j"),
+                1.0,
+                0.0,
+                mybir.AluOpType.mult,
+                mybir.AluOpType.add,
             )
 
         def quantize_part(name, e, part):
@@ -222,10 +237,11 @@ def tile_moe_duo_s_gelu_kernel(
         gather_planes(0)
         scalar_matrix("w1", 0)
         scalar_matrix("w1", 1)
-        gather_planes(1, "grouped_w1_1_0")
-        round_part("w1", 2, (0, WIDTH), SHARE, WIDTH - SHARE, on_scalar)
-        round_part("w1", 2, (0, WIDTH), 0, SHARE, on_vector)
-        quantize_part("w1", 2, (0, WIDTH))
+        gather_planes(1)
+        round_part("w1", 2, low, 0, 2 * M, on_scalar)
+        round_on_gpsimd("w1", 2, high)
+        quantize_part("w1", 2, low)
+        quantize_part("w1", 2, high)
         first_layer(0, token_first, (0, 1))
         first_layer(1, partner_first, (2, 5))
         turn_hidden(0, 3)

@@ -57,10 +57,7 @@ def tile_moe_duo_s_gelu_kernel(
         nc.vector.memset(warm[:, :8], 0)
         nc.scalar.activation(warm[:, 8:], warm[:, :8], GELU)
         nc.vector.memset(x_codes[:, T:], 0)
-        nc.gpsimd.memset(wp_plane[:].bitcast(I32), 0)
-        wp_rows = wp_scales.bitcast(I32).rearrange("e s (q r) c -> r q (e s) c", r=4)
-        for r in range(4):
-            nc.gpsimd.dma_start(wp_plane[:].bitcast(I32)[r:P:32, :, :], wp_rows[r])
+        nc.vector.memset(wp_plane[:].bitcast(I32), 0)
         make_identity(nc, identity[:])
 
         weights = {"w1": w1, "w2": w2}
@@ -81,6 +78,9 @@ def tile_moe_duo_s_gelu_kernel(
             load_matrix("w1", e)
         wp_by_partition = wp_words.bitcast(I32).rearrange("e s p c -> p (e s) c")
         nc.sync.dma_start(wp_pair[0][:].bitcast(I32), wp_by_partition[:, :2, :])
+        wp_rows = wp_scales.bitcast(I32).rearrange("e s (q r) c -> r q (e s) c", r=4)
+        for r in range(4):
+            nc.sync.dma_start(wp_plane[:].bitcast(I32)[r:P:32, :, :], wp_rows[r])
         load_matrix("w2", 0)
         nc.sync.dma_start(wp_pair[1][:].bitcast(I32), wp_by_partition[:, 2:, :])
         load_matrix("w1", E - 1)

@@ -20,6 +20,7 @@ P = 128
 PACK = 4
 M = 128
 ALIGN = 64
+DMA_ALIGN = 256
 WIDTH = 512
 WINDOW = 2 * T
 WORD_WINDOW = 1408
@@ -41,7 +42,9 @@ def tile_moe_duo_s_gelu_kernel(
         def tile(shape, dtype, name, tag=None):
             if name in placed:
                 return held.tile(shape, dtype, name=name, align_bytes=ALIGN, offset=placed[name])
-            return sb.tile(shape, dtype, name=name, tag=tag or name, align_bytes=ALIGN)
+            tag = tag or name
+            align = DMA_ALIGN if tag.startswith(("raw", "staged", "x_", "wp_")) else ALIGN
+            return sb.tile(shape, dtype, name=name, tag=tag, align_bytes=align)
 
         token_list = lists.tile([P, E * C // 16], U16, name="token_list")
         partner_list = lists.tile([P, E * C // 16], U16, name="partner_list")

@@ -25,6 +25,7 @@ WIDTH = 512
 WINDOW = 2 * T
 WORD_WINDOW = 1408
 GROUP = 2 * C
+SHARE = 192
 
 
 def tile_moe_duo_s_gelu_kernel(
@@ -34,14 +35,9 @@ def tile_moe_duo_s_gelu_kernel(
     with ExitStack() as ctx:
         lists = ctx.enter_context(tc.tile_pool(name="lists", bufs=1))
         sb = ctx.enter_context(tc.tile_pool(name="sb", bufs=1))
-        held = ctx.enter_context(tc.tile_pool(name="held", bufs=1))
         psum = ctx.enter_context(tc.psum_pool(name="psum", bufs=1))
 
-        placed = {"grouped_w1_1_0": 0, "planes_1": 0, "grouped_w1_2_256": 2 * GROUP}
-
         def tile(shape, dtype, name, tag=None):
-            if name in placed:
-                return held.tile(shape, dtype, name=name, align_bytes=ALIGN, offset=placed[name])
             tag = tag or name
             align = DMA_ALIGN if tag.startswith(("raw", "staged", "x_", "wp_")) else ALIGN
             return sb.tile(shape, dtype, name=name, tag=tag, align_bytes=align)
@@ -109,9 +105,10 @@ def tile_moe_duo_s_gelu_kernel(
 
         grouped = {}
 
-        def round_part(name, e, part, first, width, copy):
+        def round_part(name, e, part, first, width, copy, tag=None):
             if (name, e, part) not in grouped:
-                grouped[name, e, part] = tile([P, (part[1] - part[0]) * PACK], BF16, "grouped_%s_%d_%d" % (name, e, part[0]))
+                label = "grouped_%s_%d_%d" % (name, e, part[0])
+                grouped[name, e, part] = tile([P, (part[1] - part[0]) * PACK], BF16, label, tag)
             at = (first - part[0]) * PACK
             source = raw[name, e][:, :, first : first + width]
             copy(
@@ -119,11 +116,11 @@ def tile_moe_duo_s_gelu_kernel(
                 source.rearrange("p (u d) (m i) -> p m u i d", i=4, d=2),
             )
 
-        def round_on_gpsimd(name, e, part):
-            grouped[name, e, part] = tile([P, (part[1] - part[0]) * PACK], BF16, "grouped_%s_%d_%d" % (name, e, part[0]))
+        def round_on_gpsimd(name, e, part, width):
+            at = (part[1] - part[0] - width) * PACK
             nc.gpsimd.tensor_scalar(
-                grouped[name, e, part][:].rearrange("p (c j) -> p c j", j=PACK),
-                raw[name, e][:, :, part[0] : part[1]].rearrange("p j c -> p c j"),
+                grouped[name, e, part][:, at:].rearrange("p (c j) -> p c j", j=PACK),
+                raw[name, e][:, :, part[1] - width : part[1]].rearrange("p j c -> p c j"),
                 1.0,
                 0.0,
                 mybir.AluOpType.mult,
@@ -138,10 +135,6 @@ def tile_moe_duo_s_gelu_kernel(
             nc.vector.quantize_mx(
                 out=codes[name, e][:, cols].bitcast(FP8X4), scales=scales[name, e][:, cols], in_=grouped[name, e, part][:]
             )
-
-        def scalar_matrix(name, e):
-            round_part(name, e, (0, WIDTH), 0, WIDTH, nc.scalar.copy)
-            quantize_part(name, e, (0, WIDTH))
 
         def vector_matrix(name, e, parts):
             for part in parts:
@@ -237,12 +230,15 @@ def tile_moe_duo_s_gelu_kernel(
         low, high = (0, 2 * M), (2 * M, 4 * M)
         quarters = [(u * M, (u + 1) * M) for u in range(PACK)]
         gather_words()
-        gather_planes(0)
-        scalar_matrix("w1", 0)
-        scalar_matrix("w1", 1)
-        gather_planes(1)
+        whole = (0, WIDTH)
+        for e in range(2):
+            round_part("w1", e, whole, 0, WIDTH - M, on_scalar, "grouped_w1")
+            round_on_gpsimd("w1", e, whole, M)
+            quantize_part("w1", e, whole)
+            gather_planes(e, "raw_w1_%d" % e)
         round_part("w1", 2, low, 0, 2 * M, on_scalar)
-        round_on_gpsimd("w1", 2, high)
+        round_part("w1", 2, high, 2 * M, 2 * M - SHARE, on_scalar, "grouped_w1")
+        round_on_gpsimd("w1", 2, high, SHARE)
         quantize_part("w1", 2, low)
         quantize_part("w1", 2, high)
         first_layer(0, token_first, (0, 1))

@@ -144,8 +144,7 @@ def tile_moe_duo_s_gelu_kernel(
 
         by_slot = {}
 
-        def first_layer(e, sides, banks, tag=None):
-            by_slot[e] = tile([P, 2 * H], BF16, "by_slot_%d" % e, tag)
+        def first_layer(e, sides, banks, tags=(None, None)):
             moving = (
                 (codes["w1", e][:].bitcast(FP8X4), scales["w1", e][:]),
                 (wp_codes[e].bitcast(FP4X4), wp_plane[:, e, :]),
@@ -164,8 +163,9 @@ def tile_moe_duo_s_gelu_kernel(
                         start=side == sides[0],
                         stop=side == sides[1],
                     )
+                by_slot[e, half] = tile([P, H], BF16, "by_slot_%d_%d" % (e, half), tags[half])
                 nc.scalar.activation(
-                    by_slot[e][:, half * H : (half + 1) * H].rearrange("s (u p d) -> s u p d", u=2, d=2),
+                    by_slot[e, half][:].rearrange("s (u p d) -> s u p d", u=2, d=2),
                     bank[:].rearrange("s (p u d) -> s u p d", u=2, d=2),
                     GELU,
                 )
@@ -175,13 +175,12 @@ def tile_moe_duo_s_gelu_kernel(
 
         hidden = {}
 
-        def turn_hidden(e, number, tag=None):
+        def turn_hidden(e, number, halves=(0, 1), tag=None):
             bank = psum.tile([P, 2, 2, M], F32, name="bank", tag="bank_%d" % number)
-            pairs = by_slot[e][:].bitcast(F32)
-            for half in range(C // M):
+            for half in halves:
+                pairs = by_slot[e, half][:].bitcast(F32)
                 for u in range(2):
-                    first = (2 * half + u) * P
-                    nc.tensor.transpose(bank[:, half, u, :], pairs[:, first : first + P], identity[:])
+                    nc.tensor.transpose(bank[:, half, u, :], pairs[:, u * P : (u + 1) * P], identity[:])
             hidden[e] = tile([P, C * PACK], BF16, "hidden_%d" % e, tag)
             nc.scalar.copy(
                 hidden[e][:].bitcast(F32).rearrange("p (h s u) -> p h s u", h=2, u=2),
@@ -255,8 +254,8 @@ def tile_moe_duo_s_gelu_kernel(
         second_layer(0, 0, 2, 6, on_scalar)
         second_layer(0, 2, 2, 7, on_scalar)
         store(0, 0)
-        first_layer(3, partner_first, (2, 5))
         vector_matrix("w2", 1, (low, high))
+        first_layer(3, partner_first, (2, 5), (None, "grouped_w2_1_0"))
         quantize_hidden(2, "raw_w2_1")
         stage(0, 2, 1, 1)
         stage(2, 2, 1, 1)
@@ -264,8 +263,13 @@ def tile_moe_duo_s_gelu_kernel(
         store(0, 1)
         second_layer(1, 2, 2, 1, on_scalar)
         store(2, 1)
-        turn_hidden(3, 0)
-        vector_matrix("w2", 2, (low, high))
+        turn_hidden(3, 4, (1, 0))
+        round_part("w2", 2, low, 0, 2 * M, on_vector)
+        round_part("w2", 2, quarters[2], 2 * M, M, on_vector)
+        quantize_part("w2", 2, low)
+        round_part("w2", 2, quarters[3], 3 * M, M, on_vector)
+        quantize_part("w2", 2, quarters[2])
+        quantize_part("w2", 2, quarters[3])
         stage(0, 2, 2, 1)
         stage(2, 2, 2, 1)
         second_layer(2, 0, 2, 6, on_scalar)

from contextlib import ExitStack

import concourse.mybir as mybir
from concourse.masks import make_identity

K, T, E, C, H, N = 512, 512, 4, 256, 512, 512
FLOPS = 2 * E * C * (2 * K * H + H * N)

F32 = mybir.dt.float32
BF16 = mybir.dt.bfloat16
I32 = mybir.dt.int32
U32 = mybir.dt.uint32
U16 = mybir.dt.uint16
U8 = mybir.dt.uint8
FP8X4 = mybir.dt.float8_e4m3fn_x4
FP4X4 = mybir.dt.float4_e2m1fn_x4
GELU = mybir.ActivationFunctionType.Gelu_apprx_tanh

P = 128
PACK = 4
M = 128
ALIGN = 64
DMA_ALIGN = 256
WIDTH = 512
WINDOW = 2 * T
WORD_WINDOW = 1408
GROUP = 2 * C
SHARE = 192


def tile_moe_duo_s_gelu_kernel(
    tc, x_words, x_scales, w1, wp_words, wp_scales, w2, offs, offs2, out
):
    nc = tc.nc
    with ExitStack() as ctx:
        lists = ctx.enter_context(tc.tile_pool(name="lists", bufs=1))
        sb = ctx.enter_context(tc.tile_pool(name="sb", bufs=1))
        psum = ctx.enter_context(tc.psum_pool(name="psum", bufs=1))

        def tile(shape, dtype, name, tag=None):
            tag = tag or name
            align = DMA_ALIGN if tag.startswith(("raw", "staged", "x_", "wp_")) else ALIGN
            return sb.tile(shape, dtype, name=name, tag=tag, align_bytes=align)

        token_list = lists.tile([P, E * C // 16], U16, name="token_list")
        partner_list = lists.tile([P, E * C // 16], U16, name="partner_list")
        x_codes = tile([P, WORD_WINDOW], I32, "x_codes")
        x_plane = tile([P, WINDOW], U8, "x_plane")
        wp_pair = [tile([P, 2, 2 * H], U8, "wp_pair_%d" % g) for g in range(2)]
        wp_codes = [wp_pair[e // 2][:, e % 2, :] for e in range(E)]
        wp_plane = tile([P, E, H], U8, "wp_plane")
        identity = tile([P, P], F32, "identity")

        nc.vector.memset(x_plane[:].bitcast(I32), 0)
        warm = tile([P, 16], F32, "warm")
        nc.vector.memset(warm[:, :8], 0)
        nc.scalar.activation(warm[:, 8:], warm[:, :8], GELU)
        nc.vector.memset(x_codes[:, T:], 0)
        nc.vector.memset(wp_plane[:].bitcast(I32), 0)
        make_identity(nc, identity[:])

        weights = {"w1": w1, "w2": w2}
        raw = {}

        def load_matrix(name, e):
            raw[name, e] = tile([P, PACK, WIDTH], F32, "raw_%s_%d" % (name, e))
            nc.sync.dma_start(raw[name, e][:], weights[name][e].rearrange("(p j) c -> p j c", j=PACK))

        nc.sync.dma_start(x_codes[:, :T], x_words[0].rearrange("p t d -> p (t d)").bitcast(I32))
        nc.sync.dma_start(token_list[:], offs)
        nc.sync.dma_start(partner_list[:], offs2)
        load_matrix("w1", 0)
        x_rows = x_scales[0].bitcast(I32).rearrange("(q r) c -> r q c", r=4)
        for r in range(4):
            nc.sync.dma_start(x_plane[:].bitcast(I32)[r:P:32, : T // 4], x_rows[r])
        for e in range(1, E - 1):
            load_matrix("w1", e)
        wp_by_partition = wp_words.bitcast(I32).rearrange("e s p c -> p (e s) c")
        nc.sync.dma_start(wp_pair[0][:].bitcast(I32), wp_by_partition[:, :2, :])
        wp_rows = wp_scales.bitcast(I32).rearrange("e s (q r) c -> r q (e s) c", r=4)
        for r in range(4):
            nc.sync.dma_start(wp_plane[:].bitcast(I32)[r:P:32, :, :], wp_rows[r])
        load_matrix("w2", 0)
        nc.sync.dma_start(wp_pair[1][:].bitcast(I32), wp_by_partition[:, 2:, :])
        load_matrix("w1", E - 1)
        for e in range(1, E):
            load_matrix("w2", e)

        words = {}
        planes = {}

        def gather_words():
            for s, lst in enumerate((token_list, partner_list)):
                words[s] = tile([P, E * C], U32, "words_%d" % s)
                nc.vector.tensor_copy(words[s][:], x_codes[:].bitcast(U32).indirect(lst[:]))

        def gather_planes(g, tag=None):
            planes[g] = tile([P, 2, GROUP], U8, "planes_%d" % g, tag)
            for s, lst in enumerate((token_list, partner_list)):
                offsets = lst[:, g * GROUP // 16 : (g + 1) * GROUP // 16]
                nc.vector.tensor_copy(planes[g][:, s, :], x_plane[:].indirect(offsets))

        codes = {}
        scales = {}

        grouped = {}

        def round_part(name, e, part, first, width, copy, tag=None):
            if (name, e, part) not in grouped:
                label = "grouped_%s_%d_%d" % (name, e, part[0])
                grouped[name, e, part] = tile([P, (part[1] - part[0]) * PACK], BF16, label, tag)
            at = (first - part[0]) * PACK
            source = raw[name, e][:, :, first : first + width]
            copy(
                grouped[name, e, part][:, at : at + width * PACK].rearrange("p (m i u d) -> p m u i d", i=4, u=2, d=2),
                source.rearrange("p (u d) (m i) -> p m u i d", i=4, d=2),
            )

        def round_on_gpsimd(name, e, part, width):
            at = (part[1] - part[0] - width) * PACK
            nc.gpsimd.tensor_scalar(
                grouped[name, e, part][:, at:].rearrange("p (c j) -> p c j", j=PACK),
                raw[name, e][:, :, part[1] - width : part[1]].rearrange("p j c -> p c j"),
                1.0,
                0.0,
                mybir.AluOpType.mult,
                mybir.AluOpType.add,
            )

        def quantize_part(name, e, part):
            if (name, e) not in codes:
                codes[name, e] = tile([P, WIDTH], U32, "codes_%s_%d" % (name, e))
                scales[name, e] = tile([P, WIDTH], U8, "scales_%s_%d" % (name, e))
            cols = slice(part[0], part[1])
            nc.vector.quantize_mx(
                out=codes[name, e][:, cols].bitcast(FP8X4), scales=scales[name, e][:, cols], in_=grouped[name, e, part][:]
            )

        def vector_matrix(name, e, parts):
            for part in parts:
                round_part(name, e, part, part[0], part[1] - part[0], nc.vector.tensor_copy)
            for part in parts:
                quantize_part(name, e, part)

        by_slot = {}

        def first_layer(e, sides, banks, tags=(None, None)):
            moving = (
                (codes["w1", e][:].bitcast(FP8X4), scales["w1", e][:]),
                (wp_codes[e].bitcast(FP4X4), wp_plane[:, e, :]),
            )
            for half in range(C // M):
                first = (e % 2) * C + half * M
                slots = slice(first, first + M)
                bank = psum.tile([P, H], F32, name="bank", tag="bank_%d" % banks[half])
                for side in sides:
                    nc.tensor.matmul_mx(
                        out=bank[:],
                        lhsT=words[side][:, e * C + half * M : e * C + (half + 1) * M].bitcast(FP8X4),
                        lhsT_scale=planes[e // 2][:, side, slots],
                        rhs=moving[side][0],
                        rhs_scale=moving[side][1],
                        start=side == sides[0],
                        stop=side == sides[1],
                    )
                by_slot[e, half] = tile([P, H], BF16, "by_slot_%d_%d" % (e, half), tags[half])
                nc.scalar.activation(
                    by_slot[e, half][:].rearrange("s (u p d) -> s u p d", u=2, d=2),
                    bank[:].rearrange("s (p u d) -> s u p d", u=2, d=2),
                    GELU,
                )

        h_codes = {}
        h_scales = {}

        hidden = {}

        def turn_hidden(e, number, halves=(0, 1), tag=None):
            bank = psum.tile([P, 2, 2, M], F32, name="bank", tag="bank_%d" % number)
            for half in halves:
                pairs = by_slot[e, half][:].bitcast(F32)
                for u in range(2):
                    nc.tensor.transpose(bank[:, half, u, :], pairs[:, u * P : (u + 1) * P], identity[:])
            hidden[e] = tile([P, C * PACK], BF16, "hidden_%d" % e, tag)
            nc.scalar.copy(
                hidden[e][:].bitcast(F32).rearrange("p (h s u) -> p h s u", h=2, u=2),
                bank[:].rearrange("p h u s -> p h s u"),
            )

        def quantize_hidden(e, codes_tag):
            h_codes[e] = tile([P, C], U32, "h_codes_%d" % e, codes_tag)
            h_scales[e] = tile([P, C], U8, "h_scales_%d" % e)
            nc.vector.quantize_mx(out=h_codes[e][:].bitcast(FP8X4), scales=h_scales[e][:], in_=hidden[e][:])

        out_view = out.rearrange("(u p) c -> p u c", p=P)

        staged = {}

        def stage(first, count, first_expert, experts, tag=None):
            rows = tile([P, count, experts * C], F32, "staged_%d_%d" % (first, first_expert), tag)
            for u in range(first, first + count):
                for e in range(first_expert, first_expert + experts):
                    staged[u, e] = (rows, first, first_expert)

        def second_layer(e, first, count, number, copy):
            bank = psum.tile([P, count, C], F32, name="bank", tag="bank_%d" % number)
            for i in range(count):
                cols = slice((first + i) * M, (first + i + 1) * M)
                nc.tensor.matmul_mx(
                    out=bank[:, i, :],
                    lhsT=codes["w2", e][:, cols].bitcast(FP8X4),
                    lhsT_scale=scales["w2", e][:, cols],
                    rhs=h_codes[e][:].bitcast(FP8X4),
                    rhs_scale=h_scales[e][:],
                    start=True,
                    stop=True,
                )
            rows, row_0, expert_0 = staged[first, e]
            at = (e - expert_0) * C
            copy(rows[:, first - row_0 : first - row_0 + count, at : at + C], bank[:])

        def store(first, e):
            rows, row_0, expert_0 = staged[first, e]
            count, width = rows.shape[1], rows.shape[2]
            nc.sync.dma_start(out_view[:, row_0 : row_0 + count, expert_0 * C : expert_0 * C + width], rows[:])

        on_scalar, on_vector = nc.scalar.copy, nc.vector.tensor_copy
        token_first, partner_first = (0, 1), (1, 0)
        low, high = (0, 2 * M), (2 * M, 4 * M)
        quarters = [(u * M, (u + 1) * M) for u in range(PACK)]
        gather_words()
        whole = (0, WIDTH)
        for e in range(2):
            round_part("w1", e, whole, 0, WIDTH - M, on_scalar, "grouped_w1")
            round_on_gpsimd("w1", e, whole, M)
            quantize_part("w1", e, whole)
            gather_planes(e, "raw_w1_%d" % e)
        round_part("w1", 2, low, 0, 2 * M, on_scalar)
        round_part("w1", 2, high, 2 * M, 2 * M - SHARE, on_scalar, "grouped_w1")
        round_on_gpsimd("w1", 2, high, SHARE)
        quantize_part("w1", 2, low)
        quantize_part("w1", 2, high)
        first_layer(0, token_first, (0, 1))
        first_layer(1, partner_first, (2, 5))
        turn_hidden(0, 3)
        vector_matrix("w2", 0, (low, high))
        quantize_hidden(0, "raw_w2_0")
        first_layer(2, partner_first, (0, 1))
        turn_hidden(1, 4)
        vector_matrix("w1", 3, (low, high))
        quantize_hidden(1, "raw_w1_3")
        turn_hidden(2, 3)
        stage(0, 4, 0, 1)
        second_layer(0, 0, 2, 6, on_scalar)
        second_layer(0, 2, 2, 7, on_scalar)
        store(0, 0)
        vector_matrix("w2", 1, (low, high))
        first_layer(3, partner_first, (2, 5), (None, "grouped_w2_1_0"))
        quantize_hidden(2, "raw_w2_1")
        stage(0, 2, 1, 1)
        stage(2, 2, 1, 1)
        second_layer(1, 0, 2, 0, on_scalar)
        store(0, 1)
        second_layer(1, 2, 2, 1, on_scalar)
        store(2, 1)
        turn_hidden(3, 4, (1, 0))
        round_part("w2", 2, low, 0, 2 * M, on_vector)
        round_part("w2", 2, quarters[2], 2 * M, M, on_vector)
        quantize_part("w2", 2, low)
        round_part("w2", 2, quarters[3], 3 * M, M, on_vector)
        quantize_part("w2", 2, quarters[2])
        quantize_part("w2", 2, quarters[3])
        stage(0, 2, 2, 1)
        stage(2, 2, 2, 1)
        second_layer(2, 0, 2, 6, on_scalar)
        store(0, 2)
        second_layer(2, 2, 2, 7, on_scalar)
        store(2, 2)
        for u in range(PACK):
            round_part("w2", 3, quarters[u], u * M, M, on_vector)
            if u > 0:
                quantize_part("w2", 3, quarters[u - 1])
            if u == 1:
                quantize_hidden(3, "grouped_w2_3_0")
        quantize_part("w2", 3, quarters[3])
        stage(0, 1, 3, 1)
        stage(1, 1, 3, 1)
        stage(2, 1, 3, 1)
        stage(3, 1, 3, 1)
        second_layer(3, 0, 1, 2, on_scalar)
        store(0, 3)
        second_layer(3, 1, 1, 5, on_scalar)
        store(1, 3)
        second_layer(3, 2, 1, 3, on_vector)
        store(2, 3)
        second_layer(3, 3, 1, 4, on_scalar)
        store(3, 3)
